import numpy as np
import ml_dtypes


def mxq(x, axis, fmt="e4m3"):
    dtype, down = {"e4m3": (ml_dtypes.float8_e4m3fn, 7), "e5m2": (ml_dtypes.float8_e5m2, 14)}[fmt]
    v = np.moveaxis(np.asarray(x, np.float32).astype(ml_dtypes.bfloat16).astype(np.float64), axis, -1)
    blocks = v.reshape(v.shape[:-1] + (-1, 32))
    amax = np.abs(blocks).max(-1, keepdims=True)
    byte = np.maximum(np.where(amax > 0, np.frexp(amax)[1] - 1 + 127, 0) - down, 1)
    scale = np.exp2(byte - 127.0)
    codes = (blocks / scale).astype(np.float32).astype(dtype).astype(np.float64)
    return np.moveaxis((codes * scale).reshape(v.shape), -1, axis)


WIDE = False


def mx_kscale(k):
    if not WIDE:
        return np.ones(k)
    levels = np.array([10, -10, 5, -5, 0])
    if k % 512:
        return np.exp2(np.random.permutation(np.resize(levels, k // 32))).repeat(32)
    a = np.empty((k // 512, 16))
    for p in range(k // 512):
        a[p, :8] = np.random.permutation(np.resize(levels, 8))
        for g in range(8):
            far = levels[np.abs(levels - a[p, g]) >= 10]
            a[p, g + 8] = far[np.random.randint(len(far))]
    return np.exp2(a.ravel()).repeat(32)


def f64(x):
    return np.asarray(x).astype(np.float64)


def striped(idx):
    return np.tile(idx.reshape(-1, 16).T, (8, 1)).astype(np.uint16)


def unstriped(offs):
    return offs[:16].T.reshape(-1).astype(np.int64)


E2M1 = np.array([0.0, 0.5, 1.0, 1.5, 2.0, 3.0, 4.0, 6.0, -0.0, -0.5, -1.0, -1.5, -2.0, -3.0, -4.0, -6.0])


def pack_weight(w, fmt):
    k, n = w.shape
    w = f64(np.asarray(w, np.float32).astype(ml_dtypes.bfloat16)).reshape(k // 32, 32, n)
    amax = np.abs(w).max(1)
    if fmt == "e4m3":
        byte = np.frexp(amax)[1] - 1 + 127 - 7
    else:
        mant, ex = np.frexp(amax / 6.0)
        byte = np.where(mant > 0.5, ex, ex - 1) + 127
    byte = np.clip(np.where(amax > 0, byte, 1), 1, 254)
    scaled = (w * np.exp2(127.0 - byte)[:, None, :]).reshape(k, n).astype(np.float32)
    by_word = np.ascontiguousarray(scaled.reshape(k // 512, 128, 4, n).transpose(0, 1, 3, 2))
    if fmt == "e4m3":
        words = by_word.astype(ml_dtypes.float8_e4m3fn).view(np.uint8)
    else:
        c = by_word.astype(ml_dtypes.float4_e2m1fn).view(np.uint8) & 0xF
        words = (c[..., 0::2] | (c[..., 1::2] << 4)).reshape(k // 512, 128, 2 * n)
    return np.ascontiguousarray(words), np.ascontiguousarray(byte.astype(np.uint8).reshape(k // 512, 16, n))


def unpack_weight(words, scales, fmt):
    g, _, n = scales.shape
    words = np.ascontiguousarray(words).reshape(g, 128, n, -1)
    if fmt == "e4m3":
        vals = words.view(ml_dtypes.float8_e4m3fn).astype(np.float64)
    else:
        nib = np.empty((g, 128, n, 4), np.uint8)
        nib[..., 0::2] = words & 0xF
        nib[..., 1::2] = words >> 4
        vals = E2M1[nib]
    vals = vals * np.repeat(np.exp2(scales.astype(np.float64) - 127.0), 8, axis=1)[..., None]
    return vals.transpose(0, 1, 3, 2).reshape(g * 512, n)


def gelu(v):
    return 0.5 * v * (1.0 + np.tanh(np.sqrt(2.0 / np.pi) * (v + 0.044715 * v**3)))


K, T, E, C, H, N = 1024, 2048, 4, 256, 512, 128


def by_expert(wq, xq):
    return np.concatenate([wq[e].T @ xq[:, e * C:(e + 1) * C] for e in range(E)], axis=1)


def setup_inputs():
    n = np.random.standard_normal
    s = mx_kscale(K)[:, None]
    u = mx_kscale(H)
    w1 = [pack_weight(m, "e2m1") for m in n((E, K, H)) / np.sqrt(K) / s[None]]
    w3 = [pack_weight(m, "e2m1") for m in n((E, K, H)) / np.sqrt(K) / s[None] * u[None, None, :]]
    w2 = [pack_weight(m, "e2m1") for m in n((E, H, N)) / np.sqrt(H) / u[None, :, None]]
    x = pack_weight(n((K, T)) * s, "e4m3")
    return {
        "x_words": x[0],
        "x_scales": x[1],
        "xr": n((N, T)).astype(np.float32),
        "w1_words": np.stack([m[0] for m in w1]),
        "w1_scales": np.stack([m[1] for m in w1]),
        "w3_words": np.stack([m[0] for m in w3]),
        "w3_scales": np.stack([m[1] for m in w3]),
        "w2_words": np.stack([m[0] for m in w2]),
        "w2_scales": np.stack([m[1] for m in w2]),
        "gate": np.tile(np.random.uniform(0.2, 1.0, E * C), (N, 1)).astype(np.float32),
        "offs": striped(np.random.permutation(T)[:E * C]),
    }


def reference(x_words, x_scales, xr, w1_words, w1_scales, w3_words, w3_scales, w2_words, w2_scales, gate, offs):
    idx = unstriped(offs)
    w1 = np.stack([unpack_weight(w1_words[e], w1_scales[e], "e2m1") for e in range(E)])
    w3 = np.stack([unpack_weight(w3_words[e], w3_scales[e], "e2m1") for e in range(E)])
    w2 = np.stack([unpack_weight(w2_words[e], w2_scales[e], "e2m1") for e in range(E)])
    xq = unpack_weight(x_words, x_scales, "e4m3")[:, idx]
    h = gelu(by_expert(w1, xq))
    h = h * by_expert(w3, xq)
    y = by_expert(w2, mxq(h, 0, "e4m3"))
    out = f64(xr).copy()
    out[:, idx] += f64(gate) * y
    return out

@@ -1,0 +1,190 @@
+from contextlib import ExitStack
+
+import concourse.mybir as mybir
+from concourse.masks import make_identity
+
+K, T, E, C, H, N = 1024, 2048, 4, 256, 512, 128
+SLOTS = E * C
+FLOPS = 2 * SLOTS * H * (2 * K + N)
+
+F32 = mybir.dt.float32
+BF16 = mybir.dt.bfloat16
+I32 = mybir.dt.int32
+U32 = mybir.dt.uint32
+U16 = mybir.dt.uint16
+U8 = mybir.dt.uint8
+FP8X4 = mybir.dt.float8_e4m3fn_x4
+FP4X4 = mybir.dt.float4_e2m1fn_x4
+MULT = mybir.AluOpType.mult
+ADD = mybir.AluOpType.add
+GELU = mybir.ActivationFunctionType.Gelu_apprx_tanh
+
+P = 128
+PASSES = K // 512
+QUADS = 4
+TILES = C // P
+LIST_COLS = C // 16
+OUT_CHUNK = 512
+LIVE_ROWS = 100
+
+
+def tile_moe_res_glu_gelu_kernel(
+    tc, x_words, x_scales, xr, w1_words, w1_scales, w3_words, w3_scales, w2_words, w2_scales, gate, offs, out
+):
+    nc = tc.nc
+    with ExitStack() as ctx:
+        held = ctx.enter_context(tc.tile_pool(name="held", bufs=1))
+        ring = ctx.enter_context(tc.tile_pool(name="ring", bufs=3))
+        psum = ctx.enter_context(tc.psum_pool(name="psum", bufs=1))
+
+        offsets = held.tile([P, SLOTS // 16], U16, name="offsets")
+        nc.sync.dma_start(offsets[:], offs)
+
+        tok_words = [held.tile([P, T], I32, name="tok_words%d" % o) for o in range(PASSES)]
+        tok_scales = held.tile([P, T], U8, name="tok_scales")
+        up_words = [
+            [held.tile([P, PASSES, 2 * H], U8, name="up_words%d_%d" % (m, e), align_bytes=64) for e in range(E)]
+            for m in range(2)
+        ]
+        up_scales = [held.tile([P, E * PASSES, H], U8, name="up_scales%d" % m, align_bytes=64) for m in range(2)]
+        down_words = held.tile([P, E, 2 * N], U8, name="down_words", align_bytes=64)
+        down_scales = held.tile([P, E, N], U8, name="down_scales", align_bytes=64)
+        slot_words = [held.tile([P, SLOTS], U32, name="slot_words%d" % o, align_bytes=64) for o in range(PASSES)]
+        slot_scales = [held.tile([P, SLOTS], U8, name="slot_scales%d" % o, align_bytes=64) for o in range(PASSES)]
+        gate_sb = held.tile([P, SLOTS], F32, name="gate_sb")
+        total = held.tile([P, T], F32, name="total")
+        routed = held.tile([P, T], F32, name="routed")
+        ident = held.tile([P, P], F32, name="ident")
+        y_sb = [held.tile([P, C], F32, name="y_sb%d" % e) for e in range(E)]
+
+        nc.vector.memset(tok_scales[:].bitcast(I32), 0)
+        for m in (1, 0):
+            nc.vector.memset(up_scales[m][:].bitcast(I32), 0)
+        nc.vector.memset(slot_scales[1][:].bitcast(I32), 0)
+        nc.vector.memset(down_scales[:].bitcast(I32), 0)
+        nc.vector.memset(routed[:], 0.0)
+        make_identity(nc, ident[:])
+
+        def load_tokens(o):
+            nc.sync.dma_start(tok_words[o][:], x_words[o].rearrange("p t r -> p (t r)").bitcast(I32))
+
+        def load_up(m, e):
+            words = (w1_words, w3_words)[m]
+            nc.sync.dma_start(up_words[m][e][:].bitcast(I32), words[e].rearrange("s p b -> p s b").bitcast(I32))
+
+        def load_scale_rows(queue, plane, scales):
+            for q in range(QUADS):
+                rows = scales[:, :, 4 * q : 4 * q + 4, :].rearrange("e s r n -> r (e s) n")
+                queue.dma_start(plane[32 * q : 32 * q + 4, :, :].bitcast(I32), rows.bitcast(I32))
+
+        load_tokens(0)
+        for q in range(QUADS):
+            nc.scalar.dma_start(
+                tok_scales[32 * q : 32 * q + 8, :].bitcast(I32), x_scales[:, 4 * q : 4 * q + 4, :].bitcast(I32)
+            )
+        load_scale_rows(nc.gpsimd, up_scales[1], w3_scales)
+        load_tokens(1)
+        load_scale_rows(nc.scalar, up_scales[0], w1_scales)
+        load_up(0, 0)
+        load_up(1, 0)
+
+        def gather_scales(queue, half):
+            cols = slice(half * SLOTS // 2, (half + 1) * SLOTS // 2)
+            half_list = offsets[:, half * 2 * LIST_COLS : (half + 1) * 2 * LIST_COLS]
+            nc.vector.tensor_copy(slot_scales[0][:, cols], tok_scales[:].indirect(half_list))
+            queue.dma_start(
+                slot_scales[1][0:LIVE_ROWS, cols].bitcast(I32), slot_scales[0][4 : 4 + LIVE_ROWS, cols].bitcast(I32)
+            )
+
+        gather_scales(nc.scalar, 0)
+        load_up(0, 1)
+        load_up(1, 1)
+        load_scale_rows(nc.sync, down_scales, w2_scales)
+
+        def expert_list(e):
+            return offsets[:, e * LIST_COLS : (e + 1) * LIST_COLS]
+
+        def gather_words(o, e):
+            nc.vector.tensor_copy(
+                slot_words[o][:, e * C : (e + 1) * C], tok_words[o][:].bitcast(U32).indirect(expert_list(e))
+            )
+
+        hidden = {}
+
+        def up(e, j):
+            cols = slice(e * C + j * P, e * C + (j + 1) * P)
+            sums = [psum.tile([P, H], F32, name="sums%d" % m, bufs=2 + m) for m in range(2)]
+            for m in range(2):
+                for o in range(PASSES):
+                    nc.tensor.matmul_mx(
+                        out=sums[m][:],
+                        lhsT=slot_words[o][:, cols].bitcast(FP8X4),
+                        lhsT_scale=slot_scales[o][:, cols],
+                        rhs=up_words[m][e][:, o, :].bitcast(FP4X4),
+                        rhs_scale=up_scales[m][:, e * PASSES + o, :],
+                        start=(o == 0),
+                        stop=(o == PASSES - 1),
+                    )
+            by_pairs = [s[:].rearrange("c (p u v) -> c u p v", u=2, v=2) for s in sums]
+            act = ring.tile([P, 2, P, 2], F32, name="act")
+            nc.scalar.activation(act[:], by_pairs[0], GELU)
+            h = ring.tile([P, 2, P, 2], BF16, name="h", bufs=4)
+            nc.vector.tensor_tensor(h[:], by_pairs[1], act[:], MULT)
+            hidden[e, j] = h
+
+        def down(e):
+            turned = psum.tile([P, TILES, 2, P], F32, name="turned", bufs=2)
+            for j in range(TILES):
+                pairs = hidden[e, j][:].rearrange("c u p v -> c (u p v)").bitcast(F32)
+                for u in range(2):
+                    nc.tensor.transpose(turned[:, j, u, :], pairs[:, u * P : (u + 1) * P], ident[:])
+            h_t = ring.tile([P, 4 * C], BF16, name="h_t", bufs=2, align_bytes=64)
+            nc.scalar.copy(
+                h_t[:].bitcast(F32).rearrange("p (j c u) -> p j c u", j=TILES, u=2),
+                turned[:].rearrange("p j u c -> p j c u"),
+            )
+            h_words = ring.tile([P, C], U32, name="h_words", bufs=2, align_bytes=64)
+            h_scales = ring.tile([P, C], U8, name="h_scales", bufs=2, align_bytes=64)
+            nc.vector.quantize_mx(out=h_words[:].bitcast(FP8X4), scales=h_scales[:], in_=h_t[:])
+            y = psum.tile([P, C], F32, name="y")
+            nc.tensor.matmul_mx(
+                out=y[:],
+                lhsT=down_words[:, e, :].bitcast(FP4X4),
+                lhsT_scale=down_scales[:, e, :],
+                rhs=h_words[:].bitcast(FP8X4),
+                rhs_scale=h_scales[:],
+                start=True,
+                stop=True,
+            )
+            nc.scalar.copy(y_sb[e][:], y[:])
+
+        for e in range(2):
+            gather_words(0, e)
+        gather_words(1, 0)
+        gather_scales(nc.sync, 1)
+        gather_words(1, 1)
+        nc.sync.dma_start(down_words[:].bitcast(I32), w2_words.rearrange("e s p b -> p (e s) b").bitcast(I32))
+        nc.sync.dma_start(gate_sb[:], gate)
+        for e in range(2, E):
+            load_up(0, e)
+            load_up(1, e)
+        nc.sync.dma_start(total[:], xr)
+        for e in range(E):
+            up(e, 0)
+            if e > 0:
+                down(e - 1)
+            up(e, 1)
+            if e + 2 < E:
+                for o in range(PASSES):
+                    gather_words(o, e + 2)
+        down(E - 1)
+
+        for e in range(E):
+            nc.vector.tensor_tensor(
+                routed[:].indirect(expert_list(e)), y_sb[e][:], gate_sb[:, e * C : (e + 1) * C], MULT
+            )
+
+        for c0 in range(0, T, OUT_CHUNK):
+            cols = slice(c0, c0 + OUT_CHUNK)
+            nc.vector.tensor_tensor(total[:, cols], routed[:, cols], total[:, cols], ADD)
+            nc.sync.dma_start(out[:, cols], total[:, cols])

@@ -46,7 +46,10 @@ def tile_moe_res_glu_gelu_kernel(
             [held.tile([P, PASSES, 2 * H], U8, name="up_words%d_%d" % (m, e), align_bytes=64) for e in range(E)]
             for m in range(2)
         ]
-        up_scales = [held.tile([P, E * PASSES, H], U8, name="up_scales%d" % m, align_bytes=64) for m in range(2)]
+        w1_planes = held.tile([P, E * PASSES, H], U8, name="w1_planes", align_bytes=64)
+        w3_first = held.tile([P, PASSES, H], U8, name="w3_first", align_bytes=64)
+        w3_later = held.tile([P, (E - 1) * PASSES, H], U8, name="w3_later", align_bytes=64)
+        zero = held.tile([P, 1], F32, name="zero")
         down_words = held.tile([P, E, 2 * N], U8, name="down_words", align_bytes=64)
         down_scales = held.tile([P, E, N], U8, name="down_scales", align_bytes=64)
         slot_words = [held.tile([P, SLOTS], U32, name="slot_words%d" % o, align_bytes=64) for o in range(PASSES)]
@@ -58,35 +61,40 @@ def tile_moe_res_glu_gelu_kernel(
         y_sb = [held.tile([P, C], F32, name="y_sb%d" % e) for e in range(E)]
 
         nc.vector.memset(tok_scales[:].bitcast(I32), 0)
-        for m in (1, 0):
-            nc.vector.memset(up_scales[m][:].bitcast(I32), 0)
+        nc.vector.memset(zero[:], 0.0)
+        nc.vector.memset(w1_planes[:].bitcast(I32), 0)
         nc.vector.memset(slot_scales[1][:].bitcast(I32), 0)
+        nc.vector.memset(w3_later[:].bitcast(I32), 0)
         nc.vector.memset(down_scales[:].bitcast(I32), 0)
-        nc.vector.memset(routed[:], 0.0)
+        nc.vector.memset(w3_first[:].bitcast(I32), 0)
+        nc.scalar.activation(routed[:], zero[:].to_broadcast([P, T]), GELU)
         make_identity(nc, ident[:])
 
         def load_tokens(o):
             nc.sync.dma_start(tok_words[o][:], x_words[o].rearrange("p t r -> p (t r)").bitcast(I32))
 
-        def load_up(m, e):
-            words = (w1_words, w3_words)[m]
-            nc.sync.dma_start(up_words[m][e][:].bitcast(I32), words[e].rearrange("s p b -> p s b").bitcast(I32))
+        def load_up(m, e, passes=slice(0, PASSES)):
+            words = (w1_words, w3_words)[m][e].rearrange("s p b -> p s b")
+            nc.sync.dma_start(up_words[m][e][:, passes, :].bitcast(I32), words[:, passes, :].bitcast(I32))
 
         def load_scale_rows(queue, plane, scales):
-            for q in range(QUADS):
-                rows = scales[:, :, 4 * q : 4 * q + 4, :].rearrange("e s r n -> r (e s) n")
-                queue.dma_start(plane[32 * q : 32 * q + 4, :, :].bitcast(I32), rows.bitcast(I32))
+            rows = scales.rearrange("e s (q r) n -> r q (e s) n", r=4)
+            for r in range(4):
+                queue.dma_start(plane[r:P:32, :, :].bitcast(I32), rows[r].bitcast(I32))
 
-        load_tokens(0)
+        for m in range(2):
+            load_up(m, 0, slice(0, 1))
         for q in range(QUADS):
-            nc.scalar.dma_start(
+            nc.sync.dma_start(
                 tok_scales[32 * q : 32 * q + 8, :].bitcast(I32), x_scales[:, 4 * q : 4 * q + 4, :].bitcast(I32)
             )
-        load_scale_rows(nc.gpsimd, up_scales[1], w3_scales)
+        load_tokens(0)
+        load_scale_rows(nc.gpsimd, w1_planes[:], w1_scales)
+        load_scale_rows(nc.gpsimd, down_scales[:], w2_scales)
+        load_scale_rows(nc.scalar, w3_first[:], w3_scales[0:1])
         load_tokens(1)
-        load_scale_rows(nc.scalar, up_scales[0], w1_scales)
-        load_up(0, 0)
-        load_up(1, 0)
+        for m in range(2):
+            load_up(m, 0, slice(1, 2))
 
         def gather_scales(queue, half):
             cols = slice(half * SLOTS // 2, (half + 1) * SLOTS // 2)
@@ -96,10 +104,22 @@ def tile_moe_res_glu_gelu_kernel(
                 slot_scales[1][0:LIVE_ROWS, cols].bitcast(I32), slot_scales[0][4 : 4 + LIVE_ROWS, cols].bitcast(I32)
             )
 
-        gather_scales(nc.scalar, 0)
-        load_up(0, 1)
-        load_up(1, 1)
-        load_scale_rows(nc.sync, down_scales, w2_scales)
+        for half in range(2):
+            gather_scales(nc.scalar, half)
+        load_scale_rows(nc.scalar, w3_later[:], w3_scales[1:E])
+        for e in range(1, 3):
+            load_up(0, e)
+            load_up(1, e)
+        nc.sync.dma_start(down_words[:].bitcast(I32), w2_words.rearrange("e s p b -> p (e s) b").bitcast(I32))
+        nc.sync.dma_start(gate_sb[:], gate)
+        load_up(0, 3)
+        load_up(1, 3)
+        nc.sync.dma_start(total[:], xr)
+
+        def up_scale(m, e, o):
+            if m == 0:
+                return w1_planes[:, e * PASSES + o, :]
+            return w3_first[:, o, :] if e == 0 else w3_later[:, (e - 1) * PASSES + o, :]
 
         def expert_list(e):
             return offsets[:, e * LIST_COLS : (e + 1) * LIST_COLS]
@@ -113,7 +133,7 @@ def tile_moe_res_glu_gelu_kernel(
 
         def up(e, j):
             cols = slice(e * C + j * P, e * C + (j + 1) * P)
-            sums = [psum.tile([P, H], F32, name="sums%d" % m, bufs=2 + m) for m in range(2)]
+            sums = [psum.tile([P, H], F32, name="sums%d" % m, bufs=2 + 2 * m) for m in range(2)]
             for m in range(2):
                 for o in range(PASSES):
                     nc.tensor.matmul_mx(
@@ -121,19 +141,21 @@ def tile_moe_res_glu_gelu_kernel(
                         lhsT=slot_words[o][:, cols].bitcast(FP8X4),
                         lhsT_scale=slot_scales[o][:, cols],
                         rhs=up_words[m][e][:, o, :].bitcast(FP4X4),
-                        rhs_scale=up_scales[m][:, e * PASSES + o, :],
+                        rhs_scale=up_scale(m, e, o),
                         start=(o == 0),
                         stop=(o == PASSES - 1),
                     )
             by_pairs = [s[:].rearrange("c (p u v) -> c u p v", u=2, v=2) for s in sums]
-            act = ring.tile([P, 2, P, 2], F32, name="act")
+            act = ring.tile([P, 2, P, 2], F32, name="act", bufs=4)
             nc.scalar.activation(act[:], by_pairs[0], GELU)
-            h = ring.tile([P, 2, P, 2], BF16, name="h", bufs=4)
+            h = ring.tile([P, 2, P, 2], BF16, name="h", bufs=6)
             nc.vector.tensor_tensor(h[:], by_pairs[1], act[:], MULT)
             hidden[e, j] = h
 
-        def down(e):
-            turned = psum.tile([P, TILES, 2, P], F32, name="turned", bufs=2)
+        quantised = {}
+
+        def turn(e):
+            turned = psum.tile([P, TILES, 2, P], F32, name="turned")
             for j in range(TILES):
                 pairs = hidden[e, j][:].rearrange("c u p v -> c (u p v)").bitcast(F32)
                 for u in range(2):
@@ -146,6 +168,10 @@ def tile_moe_res_glu_gelu_kernel(
             h_words = ring.tile([P, C], U32, name="h_words", bufs=2, align_bytes=64)
             h_scales = ring.tile([P, C], U8, name="h_scales", bufs=2, align_bytes=64)
             nc.vector.quantize_mx(out=h_words[:].bitcast(FP8X4), scales=h_scales[:], in_=h_t[:])
+            quantised[e] = h_words, h_scales
+
+        def down(e):
+            h_words, h_scales = quantised[e]
             y = psum.tile([P, C], F32, name="y")
             nc.tensor.matmul_mx(
                 out=y[:],
@@ -156,33 +182,22 @@ def tile_moe_res_glu_gelu_kernel(
                 start=True,
                 stop=True,
             )
-            nc.scalar.copy(y_sb[e][:], y[:])
+            nc.vector.tensor_tensor(y_sb[e][:], y[:], gate_sb[:, e * C : (e + 1) * C], MULT)
+            nc.vector.tensor_copy(routed[:].indirect(expert_list(e)), y_sb[e][:])
 
-        for e in range(2):
-            gather_words(0, e)
-        gather_words(1, 0)
-        gather_scales(nc.sync, 1)
-        gather_words(1, 1)
-        nc.sync.dma_start(down_words[:].bitcast(I32), w2_words.rearrange("e s p b -> p (e s) b").bitcast(I32))
-        nc.sync.dma_start(gate_sb[:], gate)
-        for e in range(2, E):
-            load_up(0, e)
-            load_up(1, e)
-        nc.sync.dma_start(total[:], xr)
+        for o in range(PASSES):
+            for e in range(E):
+                gather_words(o, e)
         for e in range(E):
-            up(e, 0)
-            if e > 0:
-                down(e - 1)
-            up(e, 1)
-            if e + 2 < E:
-                for o in range(PASSES):
-                    gather_words(o, e + 2)
+            for j in range(TILES):
+                up(e, j)
+            if e >= 1:
+                turn(e - 1)
+            if e >= 2:
+                down(e - 2)
+        turn(E - 1)
+        down(E - 2)
         down(E - 1)
-
-        for e in range(E):
-            nc.vector.tensor_tensor(
-                routed[:].indirect(expert_list(e)), y_sb[e][:], gate_sb[:, e * C : (e + 1) * C], MULT
-            )
 
         for c0 in range(0, T, OUT_CHUNK):
             cols = slice(c0, c0 + OUT_CHUNK)

@@ -46,9 +46,7 @@ def tile_moe_res_glu_gelu_kernel(
             [held.tile([P, PASSES, 2 * H], U8, name="up_words%d_%d" % (m, e), align_bytes=64) for e in range(E)]
             for m in range(2)
         ]
-        w1_planes = held.tile([P, E * PASSES, H], U8, name="w1_planes", align_bytes=64)
-        w3_first = held.tile([P, PASSES, H], U8, name="w3_first", align_bytes=64)
-        w3_later = held.tile([P, (E - 1) * PASSES, H], U8, name="w3_later", align_bytes=64)
+        up_scales = [held.tile([P, E * PASSES, H], U8, name="up_scales%d" % m, align_bytes=64) for m in range(2)]
         zero = held.tile([P, 1], F32, name="zero")
         down_words = held.tile([P, E, 2 * N], U8, name="down_words", align_bytes=64)
         down_scales = held.tile([P, E, N], U8, name="down_scales", align_bytes=64)
@@ -62,64 +60,44 @@ def tile_moe_res_glu_gelu_kernel(
 
         nc.vector.memset(tok_scales[:].bitcast(I32), 0)
         nc.vector.memset(zero[:], 0.0)
-        nc.vector.memset(w1_planes[:].bitcast(I32), 0)
-        nc.vector.memset(slot_scales[1][:].bitcast(I32), 0)
-        nc.vector.memset(w3_later[:].bitcast(I32), 0)
-        nc.vector.memset(down_scales[:].bitcast(I32), 0)
-        nc.vector.memset(w3_first[:].bitcast(I32), 0)
-        nc.scalar.activation(routed[:], zero[:].to_broadcast([P, T]), GELU)
+        for plane in (up_scales[0], up_scales[1], slot_scales[1], down_scales):
+            nc.vector.memset(plane[:].bitcast(I32), 0)
         make_identity(nc, ident[:])
 
         def load_tokens(o):
             nc.sync.dma_start(tok_words[o][:], x_words[o].rearrange("p t r -> p (t r)").bitcast(I32))
 
-        def load_up(m, e, passes=slice(0, PASSES)):
+        def load_up(m, e):
             words = (w1_words, w3_words)[m][e].rearrange("s p b -> p s b")
-            nc.sync.dma_start(up_words[m][e][:, passes, :].bitcast(I32), words[:, passes, :].bitcast(I32))
+            nc.sync.dma_start(up_words[m][e][:].bitcast(I32), words.bitcast(I32))
 
-        def load_scale_rows(queue, plane, scales):
+        def load_scale_rows(plane, scales):
             rows = scales.rearrange("e s (q r) n -> r q (e s) n", r=4)
             for r in range(4):
-                queue.dma_start(plane[r:P:32, :, :].bitcast(I32), rows[r].bitcast(I32))
+                nc.sync.dma_start(plane[r:P:32, :, :].bitcast(I32), rows[r].bitcast(I32))
 
-        for m in range(2):
-            load_up(m, 0, slice(0, 1))
+        def gather_scales(half):
+            cols = slice(half * SLOTS // 2, (half + 1) * SLOTS // 2)
+            half_list = offsets[:, half * 2 * LIST_COLS : (half + 1) * 2 * LIST_COLS]
+            nc.vector.tensor_copy(slot_scales[0][:, cols], tok_scales[:].indirect(half_list))
+            nc.sync.dma_start(
+                slot_scales[1][0:LIVE_ROWS, cols].bitcast(I32), slot_scales[0][4 : 4 + LIVE_ROWS, cols].bitcast(I32)
+            )
+
+        load_up(0, 0)
         for q in range(QUADS):
             nc.sync.dma_start(
                 tok_scales[32 * q : 32 * q + 8, :].bitcast(I32), x_scales[:, 4 * q : 4 * q + 4, :].bitcast(I32)
             )
-        load_tokens(0)
-        load_scale_rows(nc.gpsimd, w1_planes[:], w1_scales)
-        load_scale_rows(nc.gpsimd, down_scales[:], w2_scales)
-        load_scale_rows(nc.scalar, w3_first[:], w3_scales[0:1])
-        load_tokens(1)
-        for m in range(2):
-            load_up(m, 0, slice(1, 2))
-
-        def gather_scales(queue, half):
-            cols = slice(half * SLOTS // 2, (half + 1) * SLOTS // 2)
-            half_list = offsets[:, half * 2 * LIST_COLS : (half + 1) * 2 * LIST_COLS]
-            nc.vector.tensor_copy(slot_scales[0][:, cols], tok_scales[:].indirect(half_list))
-            queue.dma_start(
-                slot_scales[1][0:LIVE_ROWS, cols].bitcast(I32), slot_scales[0][4 : 4 + LIVE_ROWS, cols].bitcast(I32)
-            )
-
-        for half in range(2):
-            gather_scales(nc.scalar, half)
-        load_scale_rows(nc.scalar, w3_later[:], w3_scales[1:E])
-        for e in range(1, 3):
-            load_up(0, e)
-            load_up(1, e)
-        nc.sync.dma_start(down_words[:].bitcast(I32), w2_words.rearrange("e s p b -> p (e s) b").bitcast(I32))
-        nc.sync.dma_start(gate_sb[:], gate)
-        load_up(0, 3)
-        load_up(1, 3)
-        nc.sync.dma_start(total[:], xr)
-
-        def up_scale(m, e, o):
-            if m == 0:
-                return w1_planes[:, e * PASSES + o, :]
-            return w3_first[:, o, :] if e == 0 else w3_later[:, (e - 1) * PASSES + o, :]
+        nc.scalar.activation(routed[:], zero[:].to_broadcast([P, T]), GELU)
+        for o in range(PASSES):
+            load_tokens(o)
+        gather_scales(0)
+        load_scale_rows(up_scales[0], w1_scales)
+        load_up(0, 1)
+        load_up(1, 0)
+        load_scale_rows(up_scales[1], w3_scales)
+        load_up(1, 1)
 
         def expert_list(e):
             return offsets[:, e * LIST_COLS : (e + 1) * LIST_COLS]
@@ -133,7 +111,7 @@ def tile_moe_res_glu_gelu_kernel(
 
         def up(e, j):
             cols = slice(e * C + j * P, e * C + (j + 1) * P)
-            sums = [psum.tile([P, H], F32, name="sums%d" % m, bufs=2 + 2 * m) for m in range(2)]
+            sums = [psum.tile([P, H], F32, name="sums%d" % m, bufs=3 + 2 * m) for m in range(2)]
             for m in range(2):
                 for o in range(PASSES):
                     nc.tensor.matmul_mx(
@@ -141,12 +119,12 @@ def tile_moe_res_glu_gelu_kernel(
                         lhsT=slot_words[o][:, cols].bitcast(FP8X4),
                         lhsT_scale=slot_scales[o][:, cols],
                         rhs=up_words[m][e][:, o, :].bitcast(FP4X4),
-                        rhs_scale=up_scale(m, e, o),
+                        rhs_scale=up_scales[m][:, e * PASSES + o, :],
                         start=(o == 0),
                         stop=(o == PASSES - 1),
                     )
             by_pairs = [s[:].rearrange("c (p u v) -> c u p v", u=2, v=2) for s in sums]
-            act = ring.tile([P, 2, P, 2], F32, name="act", bufs=4)
+            act = ring.tile([P, 2, P, 2], F32, name="act", bufs=5)
             nc.scalar.activation(act[:], by_pairs[0], GELU)
             h = ring.tile([P, 2, P, 2], BF16, name="h", bufs=6)
             nc.vector.tensor_tensor(h[:], by_pairs[1], act[:], MULT)
@@ -154,25 +132,27 @@ def tile_moe_res_glu_gelu_kernel(
 
         quantised = {}
 
-        def turn(e):
-            turned = psum.tile([P, TILES, 2, P], F32, name="turned")
-            for j in range(TILES):
+        def turn(e, tiles):
+            width = len(tiles) * P
+            turned = psum.tile([P, len(tiles), 2, P], F32, name="turned", tag="sums1", bufs=5)
+            for n, j in enumerate(tiles):
                 pairs = hidden[e, j][:].rearrange("c u p v -> c (u p v)").bitcast(F32)
                 for u in range(2):
-                    nc.tensor.transpose(turned[:, j, u, :], pairs[:, u * P : (u + 1) * P], ident[:])
-            h_t = ring.tile([P, 4 * C], BF16, name="h_t", bufs=2, align_bytes=64)
+                    nc.tensor.transpose(turned[:, n, u, :], pairs[:, u * P : (u + 1) * P], ident[:])
+            h_t = ring.tile([P, 4 * width], BF16, name="h_t", bufs=2, align_bytes=64)
             nc.scalar.copy(
-                h_t[:].bitcast(F32).rearrange("p (j c u) -> p j c u", j=TILES, u=2),
+                h_t[:].bitcast(F32).rearrange("p (j c u) -> p j c u", j=len(tiles), u=2),
                 turned[:].rearrange("p j u c -> p j c u"),
             )
-            h_words = ring.tile([P, C], U32, name="h_words", bufs=2, align_bytes=64)
-            h_scales = ring.tile([P, C], U8, name="h_scales", bufs=2, align_bytes=64)
+            h_words = ring.tile([P, width], U32, name="h_words", align_bytes=64)
+            h_scales = ring.tile([P, width], U8, name="h_scales", align_bytes=64)
             nc.vector.quantize_mx(out=h_words[:].bitcast(FP8X4), scales=h_scales[:], in_=h_t[:])
-            quantised[e] = h_words, h_scales
+            quantised[e, tiles] = h_words, h_scales
 
-        def down(e):
-            h_words, h_scales = quantised[e]
-            y = psum.tile([P, C], F32, name="y")
+        def down(e, tiles):
+            h_words, h_scales = quantised[e, tiles]
+            cols = slice(tiles[0] * P, (tiles[-1] + 1) * P)
+            y = psum.tile([P, len(tiles) * P], F32, name="y", tag="sums0", bufs=3)
             nc.tensor.matmul_mx(
                 out=y[:],
                 lhsT=down_words[:, e, :].bitcast(FP4X4),
@@ -182,22 +162,41 @@ def tile_moe_res_glu_gelu_kernel(
                 start=True,
                 stop=True,
             )
-            nc.vector.tensor_tensor(y_sb[e][:], y[:], gate_sb[:, e * C : (e + 1) * C], MULT)
+            nc.vector.tensor_tensor(y_sb[e][:, cols], y[:], gate_sb[:, e * C : (e + 1) * C][:, cols], MULT)
+
+        def scatter(e):
             nc.vector.tensor_copy(routed[:].indirect(expert_list(e)), y_sb[e][:])
 
-        for o in range(PASSES):
-            for e in range(E):
+        gather_words(0, 0)
+        gather_words(0, 1)
+        gather_scales(1)
+        for e in range(2, E):
+            load_up(0, e)
+            load_up(1, e)
+        load_scale_rows(down_scales, w2_scales)
+        nc.sync.dma_start(down_words[:].bitcast(I32), w2_words.rearrange("e s p b -> p (e s) b").bitcast(I32))
+        nc.sync.dma_start(gate_sb[:], gate)
+        nc.sync.dma_start(total[:], xr)
+        gather_words(1, 0)
+        gather_words(1, 1)
+        for e in range(2, E):
+            for o in range(PASSES):
                 gather_words(o, e)
+        both = tuple(range(TILES))
+        last = E - 1
         for e in range(E):
             for j in range(TILES):
                 up(e, j)
             if e >= 1:
-                turn(e - 1)
+                turn(e - 1, both)
             if e >= 2:
-                down(e - 2)
-        turn(E - 1)
-        down(E - 2)
-        down(E - 1)
+                down(e - 2, both)
+                scatter(e - 2)
+        turn(last, both)
+        down(last - 1, both)
+        down(last, both)
+        scatter(last - 1)
+        scatter(last)
 
         for c0 in range(0, T, OUT_CHUNK):
             cols = slice(c0, c0 + OUT_CHUNK)

@@ -24,7 +24,7 @@ PASSES = K // 512
 QUADS = 4
 TILES = C // P
 LIST_COLS = C // 16
-OUT_CHUNK = 512
+OUT_CUTS = (0, 512, 1024, 1536, 1792, 2048)
 LIVE_ROWS = 100
 
 
@@ -162,10 +162,12 @@ def tile_moe_res_glu_gelu_kernel(
                 start=True,
                 stop=True,
             )
-            nc.vector.tensor_tensor(y_sb[e][:, cols], y[:], gate_sb[:, e * C : (e + 1) * C][:, cols], MULT)
+            nc.scalar.copy(y_sb[e][:, cols], y[:])
 
         def scatter(e):
-            nc.vector.tensor_copy(routed[:].indirect(expert_list(e)), y_sb[e][:])
+            nc.vector.tensor_tensor(
+                routed[:].indirect(expert_list(e)), y_sb[e][:], gate_sb[:, e * C : (e + 1) * C], MULT
+            )
 
         gather_words(0, 0)
         gather_words(0, 1)
@@ -198,7 +200,7 @@ def tile_moe_res_glu_gelu_kernel(
         scatter(last - 1)
         scatter(last)
 
-        for c0 in range(0, T, OUT_CHUNK):
-            cols = slice(c0, c0 + OUT_CHUNK)
+        for c0, c1 in zip(OUT_CUTS, OUT_CUTS[1:]):
+            cols = slice(c0, c1)
             nc.vector.tensor_tensor(total[:, cols], routed[:, cols], total[:, cols], ADD)
             nc.sync.dma_start(out[:, cols], total[:, cols])

@@ -21,11 +21,11 @@ GELU = mybir.ActivationFunctionType.Gelu_apprx_tanh
 
 P = 128
 PASSES = K // 512
-QUADS = 4
 TILES = C // P
 LIST_COLS = C // 16
-OUT_CUTS = (0, 512, 1024, 1536, 1792, 2048)
+OUT_CUTS = (0, 256, 768, 1280, 1792, 2048)
 LIVE_ROWS = 100
+SHIFT = 16
 
 
 def tile_moe_res_glu_gelu_kernel(
@@ -34,7 +34,6 @@ def tile_moe_res_glu_gelu_kernel(
     nc = tc.nc
     with ExitStack() as ctx:
         held = ctx.enter_context(tc.tile_pool(name="held", bufs=1))
-        ring = ctx.enter_context(tc.tile_pool(name="ring", bufs=3))
         psum = ctx.enter_context(tc.psum_pool(name="psum", bufs=1))
 
         offsets = held.tile([P, SLOTS // 16], U16, name="offsets")
@@ -42,163 +41,214 @@ def tile_moe_res_glu_gelu_kernel(
 
         tok_words = [held.tile([P, T], I32, name="tok_words%d" % o) for o in range(PASSES)]
         tok_scales = held.tile([P, T], U8, name="tok_scales")
-        up_words = [
-            [held.tile([P, PASSES, 2 * H], U8, name="up_words%d_%d" % (m, e), align_bytes=64) for e in range(E)]
+        up_words = {
+            (m, e): held.tile([P, PASSES, 2 * H], U8, name="up_words%d_%d" % (m, e), align_bytes=64)
             for m in range(2)
-        ]
-        up_scales = [held.tile([P, E * PASSES, H], U8, name="up_scales%d" % m, align_bytes=64) for m in range(2)]
+            for e in range(E)
+            if m == 1 or e >= 2
+        }
+        w1_early = held.tile([P, 2, 2 * H], U8, name="w1_early", align_bytes=64)
+        w1_late = [held.tile([P, 2 * H], U8, name="w1_late%d" % e, align_bytes=64) for e in range(2)]
+        w1_planes = [held.tile([P, 2 * PASSES, H], U8, name="w1_planes%d" % pair, align_bytes=64) for pair in range(2)]
+        w3_planes = [held.tile([P, 2 * PASSES, H], U8, name="w3_planes%d" % pair, align_bytes=64) for pair in range(2)]
         zero = held.tile([P, 1], F32, name="zero")
         down_words = held.tile([P, E, 2 * N], U8, name="down_words", align_bytes=64)
         down_scales = held.tile([P, E, N], U8, name="down_scales", align_bytes=64)
         slot_words = [held.tile([P, SLOTS], U32, name="slot_words%d" % o, align_bytes=64) for o in range(PASSES)]
         slot_scales = [held.tile([P, SLOTS], U8, name="slot_scales%d" % o, align_bytes=64) for o in range(PASSES)]
-        gate_sb = held.tile([P, SLOTS], F32, name="gate_sb")
+        gate_sb = [held.tile([P, 2 * C], F32, name="gate_sb%d" % pair) for pair in range(2)]
         total = held.tile([P, T], F32, name="total")
         routed = held.tile([P, T], F32, name="routed")
         ident = held.tile([P, P], F32, name="ident")
+        act = [held.tile([P, 2, P, 2], F32, name="act%d" % t) for t in range(E * TILES)]
+        hidden = [held.tile([P, 2, P, 2], BF16, name="hidden%d" % t) for t in range(E * TILES)]
+        h_t = [held.tile([P, 4 * C], BF16, name="h_t%d" % e, align_bytes=64) for e in range(E)]
+        h_words = [held.tile([P, C], U32, name="h_words%d" % e, align_bytes=64) for e in range(E)]
+        h_scales = [held.tile([P, C], U8, name="h_scales%d" % e, align_bytes=64) for e in range(E)]
         y_sb = [held.tile([P, C], F32, name="y_sb%d" % e) for e in range(E)]
+        banks = [psum.tile([P, H], F32, name="bank%d" % b) for b in range(8)]
 
-        nc.vector.memset(tok_scales[:].bitcast(I32), 0)
+        nc.gpsimd.memset(tok_scales[:].bitcast(I32), 0)
         nc.vector.memset(zero[:], 0.0)
-        for plane in (up_scales[0], up_scales[1], slot_scales[1], down_scales):
+        for plane in (w1_planes[0], slot_scales[1], w3_planes[0]):
             nc.vector.memset(plane[:].bitcast(I32), 0)
+        for plane in (w1_planes[1], w3_planes[1], down_scales):
+            nc.gpsimd.memset(plane[:].bitcast(I32), 0)
         make_identity(nc, ident[:])
 
         def load_tokens(o):
             nc.sync.dma_start(tok_words[o][:], x_words[o].rearrange("p t r -> p (t r)").bitcast(I32))
 
+        def load_w1_early():
+            words = w1_words[0:2, 0].rearrange("e p b -> p e b")
+            nc.sync.dma_start(w1_early[:].bitcast(I32), words.bitcast(I32))
+
+        def load_w1_late(e):
+            nc.sync.dma_start(w1_late[e][:].bitcast(I32), w1_words[e, 1].bitcast(I32))
+
         def load_up(m, e):
             words = (w1_words, w3_words)[m][e].rearrange("s p b -> p s b")
-            nc.sync.dma_start(up_words[m][e][:].bitcast(I32), words.bitcast(I32))
+            nc.sync.dma_start(up_words[m, e][:].bitcast(I32), words.bitcast(I32))
 
-        def load_scale_rows(plane, scales):
+        def load_scale_rows(plane, scales, queue=nc.sync):
             rows = scales.rearrange("e s (q r) n -> r q (e s) n", r=4)
             for r in range(4):
-                nc.sync.dma_start(plane[r:P:32, :, :].bitcast(I32), rows[r].bitcast(I32))
+                queue.dma_start(plane[r:P:32, :, :].bitcast(I32), rows[r].bitcast(I32))
 
-        def gather_scales(half):
-            cols = slice(half * SLOTS // 2, (half + 1) * SLOTS // 2)
-            half_list = offsets[:, half * 2 * LIST_COLS : (half + 1) * 2 * LIST_COLS]
-            nc.vector.tensor_copy(slot_scales[0][:, cols], tok_scales[:].indirect(half_list))
-            nc.sync.dma_start(
-                slot_scales[1][0:LIVE_ROWS, cols].bitcast(I32), slot_scales[0][4 : 4 + LIVE_ROWS, cols].bitcast(I32)
-            )
+        def load_gate(pair):
+            nc.sync.dma_start(gate_sb[pair][:], gate[:, pair * 2 * C : (pair + 1) * 2 * C])
 
-        load_up(0, 0)
-        for q in range(QUADS):
-            nc.sync.dma_start(
-                tok_scales[32 * q : 32 * q + 8, :].bitcast(I32), x_scales[:, 4 * q : 4 * q + 4, :].bitcast(I32)
-            )
-        nc.scalar.activation(routed[:], zero[:].to_broadcast([P, T]), GELU)
-        for o in range(PASSES):
-            load_tokens(o)
-        gather_scales(0)
-        load_scale_rows(up_scales[0], w1_scales)
-        load_up(0, 1)
-        load_up(1, 0)
-        load_scale_rows(up_scales[1], w3_scales)
-        load_up(1, 1)
+        def part_list(e0, e1):
+            return offsets[:, e0 * LIST_COLS : e1 * LIST_COLS]
 
-        def expert_list(e):
-            return offsets[:, e * LIST_COLS : (e + 1) * LIST_COLS]
-
-        def gather_words(o, e):
+        def gather_words(o, e0, e1):
             nc.vector.tensor_copy(
-                slot_words[o][:, e * C : (e + 1) * C], tok_words[o][:].bitcast(U32).indirect(expert_list(e))
+                slot_words[o][:, e0 * C : e1 * C], tok_words[o][:].bitcast(U32).indirect(part_list(e0, e1))
             )
 
-        hidden = {}
+        def gather_scales(e0, e1):
+            cols = slice(e0 * C, e1 * C)
+            nc.vector.tensor_copy(slot_scales[0][:, cols], tok_scales[:].indirect(part_list(e0, e1)))
 
-        def up(e, j):
-            cols = slice(e * C + j * P, e * C + (j + 1) * P)
-            sums = [psum.tile([P, H], F32, name="sums%d" % m, bufs=3 + 2 * m) for m in range(2)]
-            for m in range(2):
-                for o in range(PASSES):
-                    nc.tensor.matmul_mx(
-                        out=sums[m][:],
-                        lhsT=slot_words[o][:, cols].bitcast(FP8X4),
-                        lhsT_scale=slot_scales[o][:, cols],
-                        rhs=up_words[m][e][:, o, :].bitcast(FP4X4),
-                        rhs_scale=up_scales[m][:, e * PASSES + o, :],
-                        start=(o == 0),
-                        stop=(o == PASSES - 1),
-                    )
-            by_pairs = [s[:].rearrange("c (p u v) -> c u p v", u=2, v=2) for s in sums]
-            act = ring.tile([P, 2, P, 2], F32, name="act", bufs=5)
-            nc.scalar.activation(act[:], by_pairs[0], GELU)
-            h = ring.tile([P, 2, P, 2], BF16, name="h", bufs=6)
-            nc.vector.tensor_tensor(h[:], by_pairs[1], act[:], MULT)
-            hidden[e, j] = h
-
-        quantised = {}
-
-        def turn(e, tiles):
-            width = len(tiles) * P
-            turned = psum.tile([P, len(tiles), 2, P], F32, name="turned", tag="sums1", bufs=5)
-            for n, j in enumerate(tiles):
-                pairs = hidden[e, j][:].rearrange("c u p v -> c (u p v)").bitcast(F32)
-                for u in range(2):
-                    nc.tensor.transpose(turned[:, n, u, :], pairs[:, u * P : (u + 1) * P], ident[:])
-            h_t = ring.tile([P, 4 * width], BF16, name="h_t", bufs=2, align_bytes=64)
-            nc.scalar.copy(
-                h_t[:].bitcast(F32).rearrange("p (j c u) -> p j c u", j=len(tiles), u=2),
-                turned[:].rearrange("p j u c -> p j c u"),
+        def move_scales(e0, e1, queue):
+            cols = slice(e0 * C, e1 * C)
+            queue.dma_start(
+                slot_scales[1][0:LIVE_ROWS, cols].bitcast(I32),
+                slot_scales[0][SHIFT : SHIFT + LIVE_ROWS, cols].bitcast(I32),
             )
-            h_words = ring.tile([P, width], U32, name="h_words", align_bytes=64)
-            h_scales = ring.tile([P, width], U8, name="h_scales", align_bytes=64)
-            nc.vector.quantize_mx(out=h_words[:].bitcast(FP8X4), scales=h_scales[:], in_=h_t[:])
-            quantised[e, tiles] = h_words, h_scales
 
-        def down(e, tiles):
-            h_words, h_scales = quantised[e, tiles]
-            cols = slice(tiles[0] * P, (tiles[-1] + 1) * P)
-            y = psum.tile([P, len(tiles) * P], F32, name="y", tag="sums0", bufs=3)
+        def up_pass(m, t, o, bank):
+            e = t // TILES
+            cols = slice(t * P, (t + 1) * P)
+            if m == 1 or e >= 2:
+                words = up_words[m, e][:, o, :]
+            else:
+                words = w1_late[e][:] if o else w1_early[:, e, :]
+            plane = (w1_planes, w3_planes)[m][e // 2][:, (e % 2) * PASSES + o, :]
             nc.tensor.matmul_mx(
-                out=y[:],
+                out=banks[bank][:],
+                lhsT=slot_words[o][:, cols].bitcast(FP8X4),
+                lhsT_scale=slot_scales[o][:, cols],
+                rhs=words.bitcast(FP4X4),
+                rhs_scale=plane,
+                start=(o == 0),
+                stop=(o == PASSES - 1),
+            )
+
+        def by_pairs(bank):
+            return banks[bank][:].rearrange("c (p u v) -> c u p v", u=2, v=2)
+
+        def gelu(t, bank):
+            nc.scalar.activation(act[t][:], by_pairs(bank), GELU)
+
+        def up1(t, bank):
+            for o in range(PASSES):
+                up_pass(0, t, o, bank)
+            gelu(t, bank)
+
+        def up3(t, bank):
+            for o in range(PASSES):
+                up_pass(1, t, o, bank)
+            nc.vector.tensor_tensor(hidden[t][:], by_pairs(bank), act[t][:], MULT)
+
+        def turn(e, bank):
+            turned = banks[bank][:].rearrange("p (j u c) -> p j u c", j=TILES, u=2)
+            for j in range(TILES):
+                pairs = hidden[e * TILES + j][:].rearrange("c u p v -> c (u p v)").bitcast(F32)
+                for u in range(2):
+                    nc.tensor.transpose(turned[:, j, u, :], pairs[:, u * P : (u + 1) * P], ident[:])
+            nc.scalar.copy(
+                h_t[e][:].bitcast(F32).rearrange("p (j c u) -> p j c u", j=TILES, u=2),
+                turned.rearrange("p j u c -> p j c u"),
+            )
+            nc.vector.quantize_mx(out=h_words[e][:].bitcast(FP8X4), scales=h_scales[e][:], in_=h_t[e][:])
+
+        def down(e, bank):
+            y = banks[bank][:, 0:C]
+            nc.tensor.matmul_mx(
+                out=y,
                 lhsT=down_words[:, e, :].bitcast(FP4X4),
                 lhsT_scale=down_scales[:, e, :],
-                rhs=h_words[:].bitcast(FP8X4),
-                rhs_scale=h_scales[:],
+                rhs=h_words[e][:].bitcast(FP8X4),
+                rhs_scale=h_scales[e][:],
                 start=True,
                 stop=True,
             )
-            nc.scalar.copy(y_sb[e][:, cols], y[:])
-
-        def scatter(e):
+            nc.scalar.copy(y_sb[e][:], y)
             nc.vector.tensor_tensor(
-                routed[:].indirect(expert_list(e)), y_sb[e][:], gate_sb[:, e * C : (e + 1) * C], MULT
+                routed[:].indirect(part_list(e, e + 1)),
+                y_sb[e][:],
+                gate_sb[e // 2][:, (e % 2) * C : (e % 2 + 1) * C],
+                MULT,
             )
 
-        gather_words(0, 0)
-        gather_words(0, 1)
-        gather_scales(1)
-        for e in range(2, E):
-            load_up(0, e)
-            load_up(1, e)
+        def load_token_scales():
+            rows = x_scales.rearrange("o (q r) t -> r q o t", r=4)
+            for r in range(4):
+                nc.sync.dma_start(tok_scales[r:P:SHIFT, :].bitcast(I32), rows[r].bitcast(I32))
+
+        def load_down():
+            nc.sync.dma_start(down_words[:].bitcast(I32), w2_words.rearrange("e s p b -> p (e s) b").bitcast(I32))
+
+        load_w1_early()
+        load_token_scales()
+        nc.scalar.activation(routed[:], zero[:].to_broadcast([P, T]), GELU)
+        load_tokens(0)
+        gather_scales(0, E)
+        load_scale_rows(w1_planes[0], w1_scales[0:2])
+        load_tokens(1)
+        move_scales(0, E, nc.sync)
+        load_w1_late(0)
+        load_scale_rows(w3_planes[0], w3_scales[0:2])
+        load_up(1, 0)
+        load_w1_late(1)
+        load_up(1, 1)
+        load_scale_rows(w1_planes[1], w1_scales[2:4])
+        load_up(1, 2)
+        load_scale_rows(w3_planes[1], w3_scales[2:4])
+        load_up(0, 2)
+        load_down()
         load_scale_rows(down_scales, w2_scales)
-        nc.sync.dma_start(down_words[:].bitcast(I32), w2_words.rearrange("e s p b -> p (e s) b").bitcast(I32))
-        nc.sync.dma_start(gate_sb[:], gate)
+        load_gate(0)
+        load_up(1, 3)
+        load_up(0, 3)
+        load_gate(1)
         nc.sync.dma_start(total[:], xr)
-        gather_words(1, 0)
-        gather_words(1, 1)
-        for e in range(2, E):
-            for o in range(PASSES):
-                gather_words(o, e)
-        both = tuple(range(TILES))
-        last = E - 1
-        for e in range(E):
-            for j in range(TILES):
-                up(e, j)
-            if e >= 1:
-                turn(e - 1, both)
-            if e >= 2:
-                down(e - 2, both)
-                scatter(e - 2)
-        turn(last, both)
-        down(last - 1, both)
-        down(last, both)
-        scatter(last - 1)
-        scatter(last)
+
+        for o in range(PASSES):
+            gather_words(o, 0, 1)
+            gather_words(o, 1, 2)
+            gather_words(o, 2, 4)
+
+        for t, bank in enumerate((0, 1, 4, 7)):
+            up_pass(0, t, 0, bank)
+        for t in range(2):
+            up_pass(0, t, 1, t)
+            gelu(t, t)
+        up3(0, 2)
+        up3(1, 3)
+        up_pass(0, 2, 1, 4)
+        gelu(2, 4)
+        up3(2, 5)
+        turn(0, 0)
+        up_pass(0, 3, 1, 7)
+        gelu(3, 7)
+        up3(3, 6)
+        up1(4, 2)
+        up3(4, 3)
+        turn(1, 2)
+        up1(5, 4)
+        up3(5, 5)
+        down(0, 0)
+        up1(6, 1)
+        up3(6, 6)
+        turn(2, 1)
+        up1(7, 7)
+        up3(7, 3)
+        down(1, 7)
+        turn(3, 4)
+        down(2, 4)
+        down(3, 5)
 
         for c0, c1 in zip(OUT_CUTS, OUT_CUTS[1:]):
             cols = slice(c0, c1)

@@ -68,12 +68,11 @@ def tile_moe_res_glu_gelu_kernel(
         y_sb = [held.tile([P, C], F32, name="y_sb%d" % e) for e in range(E)]
         banks = [psum.tile([P, H], F32, name="bank%d" % b) for b in range(8)]
 
-        nc.gpsimd.memset(tok_scales[:].bitcast(I32), 0)
-        nc.vector.memset(zero[:], 0.0)
-        for plane in (w1_planes[0], slot_scales[1], w3_planes[0]):
-            nc.vector.memset(plane[:].bitcast(I32), 0)
-        for plane in (w1_planes[1], w3_planes[1], down_scales):
+        for plane in (tok_scales, down_scales):
             nc.gpsimd.memset(plane[:].bitcast(I32), 0)
+        nc.vector.memset(zero[:], 0.0)
+        for plane in (w1_planes[0], slot_scales[1], w3_planes[0], w1_planes[1], w3_planes[1]):
+            nc.vector.memset(plane[:].bitcast(I32), 0)
         make_identity(nc, ident[:])
 
         def load_tokens(o):
@@ -194,6 +193,7 @@ def tile_moe_res_glu_gelu_kernel(
         load_token_scales()
         nc.scalar.activation(routed[:], zero[:].to_broadcast([P, T]), GELU)
         load_tokens(0)
+        load_scale_rows(down_scales, w2_scales, nc.gpsimd)
         gather_scales(0, E)
         load_scale_rows(w1_planes[0], w1_scales[0:2])
         load_tokens(1)
@@ -203,12 +203,11 @@ def tile_moe_res_glu_gelu_kernel(
         load_up(1, 0)
         load_w1_late(1)
         load_up(1, 1)
+        load_down()
         load_scale_rows(w1_planes[1], w1_scales[2:4])
         load_up(1, 2)
         load_scale_rows(w3_planes[1], w3_scales[2:4])
         load_up(0, 2)
-        load_down()
-        load_scale_rows(down_scales, w2_scales)
         load_gate(0)
         load_up(1, 3)
         load_up(0, 3)
@@ -236,18 +235,18 @@ def tile_moe_res_glu_gelu_kernel(
         up3(3, 6)
         up1(4, 2)
         up3(4, 3)
-        turn(1, 2)
+        down(0, 2)
         up1(5, 4)
         up3(5, 5)
-        down(0, 0)
+        turn(1, 4)
         up1(6, 1)
         up3(6, 6)
-        turn(2, 1)
         up1(7, 7)
+        turn(2, 1)
         up3(7, 3)
         down(1, 7)
-        turn(3, 4)
-        down(2, 4)
+        turn(3, 0)
+        down(2, 0)
         down(3, 5)
 
         for c0, c1 in zip(OUT_CUTS, OUT_CUTS[1:]):

@@ -23,9 +23,11 @@ P = 128
 PASSES = K // 512
 TILES = C // P
 LIST_COLS = C // 16
+BANKS = 8
 OUT_CUTS = (0, 256, 768, 1280, 1792, 2048)
 LIVE_ROWS = 100
 SHIFT = 16
+W1, W3 = 0, 1
 
 
 def tile_moe_res_glu_gelu_kernel(
@@ -41,129 +43,129 @@ def tile_moe_res_glu_gelu_kernel(
 
         tok_words = [held.tile([P, T], I32, name="tok_words%d" % o) for o in range(PASSES)]
         tok_scales = held.tile([P, T], U8, name="tok_scales")
-        up_words = {
-            (m, e): held.tile([P, PASSES, 2 * H], U8, name="up_words%d_%d" % (m, e), align_bytes=64)
-            for m in range(2)
-            for e in range(E)
-            if m == 1 or e >= 2
+        planes = {
+            (m, pair): held.tile([P, 2 * PASSES, H], U8, name="planes%d_%d" % (m, pair), align_bytes=64)
+            for m in (W1, W3)
+            for pair in range(2)
         }
-        w1_early = held.tile([P, 2, 2 * H], U8, name="w1_early", align_bytes=64)
-        w1_late = [held.tile([P, 2 * H], U8, name="w1_late%d" % e, align_bytes=64) for e in range(2)]
-        w1_planes = [held.tile([P, 2 * PASSES, H], U8, name="w1_planes%d" % pair, align_bytes=64) for pair in range(2)]
-        w3_planes = [held.tile([P, 2 * PASSES, H], U8, name="w3_planes%d" % pair, align_bytes=64) for pair in range(2)]
         zero = held.tile([P, 1], F32, name="zero")
         down_words = held.tile([P, E, 2 * N], U8, name="down_words", align_bytes=64)
         down_scales = held.tile([P, E, N], U8, name="down_scales", align_bytes=64)
-        slot_words = [held.tile([P, SLOTS], U32, name="slot_words%d" % o, align_bytes=64) for o in range(PASSES)]
         slot_scales = [held.tile([P, SLOTS], U8, name="slot_scales%d" % o, align_bytes=64) for o in range(PASSES)]
-        gate_sb = [held.tile([P, 2 * C], F32, name="gate_sb%d" % pair) for pair in range(2)]
         total = held.tile([P, T], F32, name="total")
         routed = held.tile([P, T], F32, name="routed")
         ident = held.tile([P, P], F32, name="ident")
-        act = [held.tile([P, 2, P, 2], F32, name="act%d" % t) for t in range(E * TILES)]
-        hidden = [held.tile([P, 2, P, 2], BF16, name="hidden%d" % t) for t in range(E * TILES)]
-        h_t = [held.tile([P, 4 * C], BF16, name="h_t%d" % e, align_bytes=64) for e in range(E)]
-        h_words = [held.tile([P, C], U32, name="h_words%d" % e, align_bytes=64) for e in range(E)]
-        h_scales = [held.tile([P, C], U8, name="h_scales%d" % e, align_bytes=64) for e in range(E)]
-        y_sb = [held.tile([P, C], F32, name="y_sb%d" % e) for e in range(E)]
-        banks = [psum.tile([P, H], F32, name="bank%d" % b) for b in range(8)]
-
-        for plane in (tok_scales, down_scales):
-            nc.gpsimd.memset(plane[:].bitcast(I32), 0)
-        nc.vector.memset(zero[:], 0.0)
-        for plane in (w1_planes[0], slot_scales[1], w3_planes[0], w1_planes[1], w3_planes[1]):
-            nc.vector.memset(plane[:].bitcast(I32), 0)
-        make_identity(nc, ident[:])
+        banks = [psum.tile([P, H], F32, name="bank%d" % b) for b in range(BANKS)]
+        up_words, slot_words, gates, sums, act, hidden, h_t, h_words, h_scales, y_sb = {}, {}, {}, {}, {}, {}, {}, {}, {}, {}
+        def zero_bytes(engine, tile):
+            engine.memset(tile[:].bitcast(I32), 0)
 
         def load_tokens(o):
             nc.sync.dma_start(tok_words[o][:], x_words[o].rearrange("p t r -> p (t r)").bitcast(I32))
 
-        def load_w1_early():
-            words = w1_words[0:2, 0].rearrange("e p b -> p e b")
-            nc.sync.dma_start(w1_early[:].bitcast(I32), words.bitcast(I32))
+        def load_token_scales():
+            rows = x_scales.rearrange("o (q r) t -> r q o t", r=4)
+            for r in range(4):
+                nc.sync.dma_start(tok_scales[r:P:SHIFT, :].bitcast(I32), rows[r].bitcast(I32))
 
-        def load_w1_late(e):
-            nc.sync.dma_start(w1_late[e][:].bitcast(I32), w1_words[e, 1].bitcast(I32))
+        def load_up(m, experts, passes):
+            src = (w1_words, w3_words)[m][experts[0] : experts[-1] + 1, passes[0] : passes[-1] + 1]
+            name = "up%d_%d_%d" % (m, experts[0], passes[0])
+            tile = held.tile([P, len(experts) * len(passes), 2 * H], U8, name=name, align_bytes=64)
+            if len(passes) == 1:
+                src = src[:, 0].rearrange("e p b -> p e b")
+            else:
+                src = src[0].rearrange("s p b -> p s b")
+            nc.sync.dma_start(tile[:].bitcast(I32), src.bitcast(I32))
+            for i, key in enumerate((m, e, o) for e in experts for o in passes):
+                up_words[key] = tile[:, i, :]
 
-        def load_up(m, e):
-            words = (w1_words, w3_words)[m][e].rearrange("s p b -> p s b")
-            nc.sync.dma_start(up_words[m, e][:].bitcast(I32), words.bitcast(I32))
-
-        def load_scale_rows(plane, scales, queue=nc.sync):
+        def load_scale_rows(plane, scales, queue):
             rows = scales.rearrange("e s (q r) n -> r q (e s) n", r=4)
             for r in range(4):
                 queue.dma_start(plane[r:P:32, :, :].bitcast(I32), rows[r].bitcast(I32))
 
-        def load_gate(pair):
-            nc.sync.dma_start(gate_sb[pair][:], gate[:, pair * 2 * C : (pair + 1) * 2 * C])
+        def load_up_scales(m, pair, queue):
+            load_scale_rows(planes[m, pair], (w1_scales, w3_scales)[m][2 * pair : 2 * pair + 2], queue)
+
+        def load_gates(e0, e1):
+            tile = held.tile([P, (e1 - e0) * C], F32, name="gate%d" % e0)
+            nc.sync.dma_start(tile[:], gate[:, e0 * C : e1 * C])
+            for e in range(e0, e1):
+                gates[e] = tile[:, (e - e0) * C : (e - e0 + 1) * C]
 
         def part_list(e0, e1):
             return offsets[:, e0 * LIST_COLS : e1 * LIST_COLS]
 
-        def gather_words(o, e0, e1):
-            nc.vector.tensor_copy(
-                slot_words[o][:, e0 * C : e1 * C], tok_words[o][:].bitcast(U32).indirect(part_list(e0, e1))
-            )
+        def gather_words(o, e0, e1, tag=None):
+            name = "slot_words%d_%d" % (o, e0)
+            tile = held.tile([P, (e1 - e0) * C], U32, name=name, tag=tag or name, align_bytes=64)
+            nc.vector.tensor_copy(tile[:], tok_words[o][:].bitcast(U32).indirect(part_list(e0, e1)))
+            for t in range(e0 * TILES, e1 * TILES):
+                slot_words[o, t] = tile[:, (t - e0 * TILES) * P : (t - e0 * TILES + 1) * P]
 
-        def gather_scales(e0, e1):
-            cols = slice(e0 * C, e1 * C)
-            nc.vector.tensor_copy(slot_scales[0][:, cols], tok_scales[:].indirect(part_list(e0, e1)))
+        def gather_scales(pair):
+            cols = slice(pair * 2 * C, (pair + 1) * 2 * C)
+            nc.vector.tensor_copy(slot_scales[0][:, cols], tok_scales[:].indirect(part_list(2 * pair, 2 * pair + 2)))
 
-        def move_scales(e0, e1, queue):
-            cols = slice(e0 * C, e1 * C)
-            queue.dma_start(
+        def move_scales(pair):
+            cols = slice(pair * 2 * C, (pair + 1) * 2 * C)
+            nc.sync.dma_start(
                 slot_scales[1][0:LIVE_ROWS, cols].bitcast(I32),
                 slot_scales[0][SHIFT : SHIFT + LIVE_ROWS, cols].bitcast(I32),
             )
 
-        def up_pass(m, t, o, bank):
+        def up_pass(m, t, o, bank=None):
             e = t // TILES
-            cols = slice(t * P, (t + 1) * P)
-            if m == 1 or e >= 2:
-                words = up_words[m, e][:, o, :]
-            else:
-                words = w1_late[e][:] if o else w1_early[:, e, :]
-            plane = (w1_planes, w3_planes)[m][e // 2][:, (e % 2) * PASSES + o, :]
+            if o == 0:
+                sums[m, t] = bank
             nc.tensor.matmul_mx(
-                out=banks[bank][:],
-                lhsT=slot_words[o][:, cols].bitcast(FP8X4),
-                lhsT_scale=slot_scales[o][:, cols],
-                rhs=words.bitcast(FP4X4),
-                rhs_scale=plane,
+                out=sums[m, t][:],
+                lhsT=slot_words[o, t].bitcast(FP8X4),
+                lhsT_scale=slot_scales[o][:, t * P : (t + 1) * P],
+                rhs=up_words[m, e, o].bitcast(FP4X4),
+                rhs_scale=planes[m, e // 2][:, (e % 2) * PASSES + o, :],
                 start=(o == 0),
                 stop=(o == PASSES - 1),
             )
 
         def by_pairs(bank):
-            return banks[bank][:].rearrange("c (p u v) -> c u p v", u=2, v=2)
+            return bank[:].rearrange("c (p u v) -> c u p v", u=2, v=2)
 
-        def gelu(t, bank):
-            nc.scalar.activation(act[t][:], by_pairs(bank), GELU)
+        def finish(m, t, tag=None):
+            up_pass(m, t, 1)
+            if m == W1:
+                act[t] = held.tile([P, 2, P, 2], F32, name="act%d" % t, align_bytes=64)
+                nc.scalar.activation(act[t][:], by_pairs(sums[m, t]), GELU)
+            else:
+                name = "hidden%d" % t
+                hidden[t] = held.tile([P, 2, P, 2], BF16, name=name, tag=tag or name, align_bytes=64)
+                nc.vector.tensor_tensor(hidden[t][:], by_pairs(sums[m, t]), act[t][:], MULT)
 
-        def up1(t, bank):
-            for o in range(PASSES):
-                up_pass(0, t, o, bank)
-            gelu(t, bank)
+        def up(m, t, bank):
+            up_pass(m, t, 0, bank)
+            finish(m, t)
 
-        def up3(t, bank):
-            for o in range(PASSES):
-                up_pass(1, t, o, bank)
-            nc.vector.tensor_tensor(hidden[t][:], by_pairs(bank), act[t][:], MULT)
-
-        def turn(e, bank):
-            turned = banks[bank][:].rearrange("p (j u c) -> p j u c", j=TILES, u=2)
-            for j in range(TILES):
-                pairs = hidden[e * TILES + j][:].rearrange("c u p v -> c (u p v)").bitcast(F32)
+        def turn(tiles, bank):
+            e = tiles[0] // TILES
+            turned = bank[:, 0 : len(tiles) * 2 * P].rearrange("p (j u c) -> p j u c", u=2, c=P)
+            for j, t in enumerate(tiles):
+                pairs = hidden[t][:].rearrange("c u p v -> c (u p v)").bitcast(F32)
                 for u in range(2):
                     nc.tensor.transpose(turned[:, j, u, :], pairs[:, u * P : (u + 1) * P], ident[:])
-            nc.scalar.copy(
-                h_t[e][:].bitcast(F32).rearrange("p (j c u) -> p j c u", j=TILES, u=2),
-                turned.rearrange("p j u c -> p j c u"),
-            )
+            if e not in h_t:
+                h_t[e] = held.tile([P, 4 * C], BF16, name="h_t%d" % e, align_bytes=64)
+            first = tiles[0] - e * TILES
+            words = h_t[e][:].bitcast(F32).rearrange("p (j c u) -> p j c u", j=TILES, u=2)
+            nc.scalar.copy(words[:, first : first + len(tiles)], turned.rearrange("p j u c -> p j c u"))
+
+        def quantize(e):
+            h_words[e] = held.tile([P, C], U32, name="h_words%d" % e, align_bytes=64)
+            h_scales[e] = held.tile([P, C], U8, name="h_scales%d" % e, align_bytes=64)
             nc.vector.quantize_mx(out=h_words[e][:].bitcast(FP8X4), scales=h_scales[e][:], in_=h_t[e][:])
 
         def down(e, bank):
-            y = banks[bank][:, 0:C]
+            y = bank[:, 0:C]
             nc.tensor.matmul_mx(
                 out=y,
                 lhsT=down_words[:, e, :].bitcast(FP4X4),
@@ -173,81 +175,75 @@ def tile_moe_res_glu_gelu_kernel(
                 start=True,
                 stop=True,
             )
+            y_sb[e] = held.tile([P, C], F32, name="y_sb%d" % e)
             nc.scalar.copy(y_sb[e][:], y)
-            nc.vector.tensor_tensor(
-                routed[:].indirect(part_list(e, e + 1)),
-                y_sb[e][:],
-                gate_sb[e // 2][:, (e % 2) * C : (e % 2 + 1) * C],
-                MULT,
-            )
+            nc.vector.tensor_tensor(routed[:].indirect(part_list(e, e + 1)), y_sb[e][:], gates[e], MULT)
 
-        def load_token_scales():
-            rows = x_scales.rearrange("o (q r) t -> r q o t", r=4)
-            for r in range(4):
-                nc.sync.dma_start(tok_scales[r:P:SHIFT, :].bitcast(I32), rows[r].bitcast(I32))
+        for plane in (tok_scales, down_scales):
+            zero_bytes(nc.gpsimd, plane)
+        nc.vector.memset(zero[:], 0.0)
+        for plane in (planes[W1, 0], slot_scales[1], planes[W3, 0], planes[W1, 1], planes[W3, 1]):
+            zero_bytes(nc.vector, plane)
+        make_identity(nc, ident[:])
 
-        def load_down():
-            nc.sync.dma_start(down_words[:].bitcast(I32), w2_words.rearrange("e s p b -> p (e s) b").bitcast(I32))
-
-        load_w1_early()
+        load_up(W1, (0, 1), (0,))
         load_token_scales()
         nc.scalar.activation(routed[:], zero[:].to_broadcast([P, T]), GELU)
         load_tokens(0)
         load_scale_rows(down_scales, w2_scales, nc.gpsimd)
-        gather_scales(0, E)
-        load_scale_rows(w1_planes[0], w1_scales[0:2])
+        for pair in range(2):
+            gather_scales(pair)
+        load_up_scales(W1, 0, nc.sync)
         load_tokens(1)
-        move_scales(0, E, nc.sync)
-        load_w1_late(0)
-        load_scale_rows(w3_planes[0], w3_scales[0:2])
-        load_up(1, 0)
-        load_w1_late(1)
-        load_up(1, 1)
-        load_down()
-        load_scale_rows(w1_planes[1], w1_scales[2:4])
-        load_up(1, 2)
-        load_scale_rows(w3_planes[1], w3_scales[2:4])
-        load_up(0, 2)
-        load_gate(0)
-        load_up(1, 3)
-        load_up(0, 3)
-        load_gate(1)
+        move_scales(0)
+        load_up(W1, (0, 1), (1,))
+        load_up_scales(W3, 0, nc.sync)
+        load_up(W3, (0,), (0, 1))
+        load_up(W3, (1,), (0, 1))
+        load_up(W1, (2,), (0, 1))
+        load_up_scales(W1, 1, nc.sync)
+        move_scales(1)
+        load_up(W3, (2,), (0, 1))
+        load_up_scales(W3, 1, nc.sync)
+        nc.sync.dma_start(down_words[:].bitcast(I32), w2_words.rearrange("e s p b -> p (e s) b").bitcast(I32))
+        load_up(W1, (3,), (0, 1))
+        load_gates(0, 1)
+        load_up(W3, (3,), (0, 1))
+        load_gates(1, E)
         nc.sync.dma_start(total[:], xr)
 
-        for o in range(PASSES):
-            gather_words(o, 0, 1)
-            gather_words(o, 1, 2)
-            gather_words(o, 2, 4)
+        for e in range(3):
+            gather_words(0, e, e + 1)
+        for e in range(E):
+            gather_words(1, e, e + 1)
 
-        for t, bank in enumerate((0, 1, 4, 7)):
-            up_pass(0, t, 0, bank)
-        for t in range(2):
-            up_pass(0, t, 1, t)
-            gelu(t, t)
-        up3(0, 2)
-        up3(1, 3)
-        up_pass(0, 2, 1, 4)
-        gelu(2, 4)
-        up3(2, 5)
-        turn(0, 0)
-        up_pass(0, 3, 1, 7)
-        gelu(3, 7)
-        up3(3, 6)
-        up1(4, 2)
-        up3(4, 3)
-        down(0, 2)
-        up1(5, 4)
-        up3(5, 5)
-        turn(1, 4)
-        up1(6, 1)
-        up3(6, 6)
-        up1(7, 7)
-        turn(2, 1)
-        up3(7, 3)
-        down(1, 7)
-        turn(3, 0)
-        down(2, 0)
-        down(3, 5)
+        for t in range(4):
+            up_pass(W1, t, 0, banks[t])
+        for t in range(4):
+            finish(W1, t)
+        for t in range(4):
+            up(W3, t, banks[4 + t])
+        gather_words(0, 3, 4, tag="up1_1_0")
+        turn((0, 1), banks[0])
+        quantize(0)
+        up(W1, 4, banks[1])
+        up(W1, 5, banks[2])
+        up(W3, 4, banks[3])
+        down(0, banks[4])
+        up(W3, 5, banks[5])
+        up(W1, 6, banks[6])
+        turn((2, 3), sums[W3, 4])
+        turn((4, 5), sums[W3, 5])
+        quantize(1)
+        quantize(2)
+        up(W1, 7, banks[7])
+        up(W3, 6, banks[0])
+        up(W3, 7, banks[1])
+        down(1, banks[2])
+        turn((6, 7), banks[6])
+        quantize(3)
+        down(2, sums[W3, 7])
+        down(3, banks[4])
 
         for c0, c1 in zip(OUT_CUTS, OUT_CUTS[1:]):
             cols = slice(c0, c1)

@@ -200,9 +200,9 @@ def tile_moe_res_glu_gelu_kernel(
         load_up_scales(W3, 0, nc.sync)
         load_up(W3, (0,), (0, 1))
         load_up(W3, (1,), (0, 1))
+        move_scales(1)
         load_up(W1, (2,), (0, 1))
         load_up_scales(W1, 1, nc.sync)
-        move_scales(1)
         load_up(W3, (2,), (0, 1))
         load_up_scales(W3, 1, nc.sync)
         nc.sync.dma_start(down_words[:].bitcast(I32), w2_words.rearrange("e s p b -> p (e s) b").bitcast(I32))
@@ -229,8 +229,8 @@ def tile_moe_res_glu_gelu_kernel(
         up(W1, 4, banks[1])
         up(W1, 5, banks[2])
         up(W3, 4, banks[3])
-        down(0, banks[4])
         up(W3, 5, banks[5])
+        down(0, banks[4])
         up(W1, 6, banks[6])
         turn((2, 3), sums[W3, 4])
         turn((4, 5), sums[W3, 5])

@@ -18,6 +18,7 @@ FP4X4 = mybir.dt.float4_e2m1fn_x4
 MULT = mybir.AluOpType.mult
 ADD = mybir.AluOpType.add
 GELU = mybir.ActivationFunctionType.Gelu_apprx_tanh
+COPY = mybir.ActivationFunctionType.Copy
 
 P = 128
 PASSES = K // 512
@@ -28,6 +29,7 @@ OUT_CUTS = (0, 256, 768, 1280, 1792, 2048)
 LIVE_ROWS = 100
 SHIFT = 16
 W1, W3 = 0, 1
+SCALE_GROUPS = ((W1, 0, 2), (W3, 0, 2), (W1, 2, 4), (W3, 2, 4))
 
 
 def tile_moe_res_glu_gelu_kernel(
@@ -44,12 +46,17 @@ def tile_moe_res_glu_gelu_kernel(
         tok_words = [held.tile([P, T], I32, name="tok_words%d" % o) for o in range(PASSES)]
         tok_scales = held.tile([P, T], U8, name="tok_scales")
         planes = {
-            (m, pair): held.tile([P, 2 * PASSES, H], U8, name="planes%d_%d" % (m, pair), align_bytes=64)
-            for m in (W1, W3)
-            for pair in range(2)
+            (m, e0): held.tile([P, (e1 - e0) * PASSES, H], U8, name="planes%d_%d" % (m, e0), align_bytes=64)
+            for m, e0, e1 in SCALE_GROUPS
+        }
+        up_scales = {
+            (m, e, o): planes[m, e0][:, (e - e0) * PASSES + o, :]
+            for m, e0, e1 in SCALE_GROUPS
+            for e in range(e0, e1)
+            for o in range(PASSES)
         }
         zero = held.tile([P, 1], F32, name="zero")
-        down_words = held.tile([P, E, 2 * N], U8, name="down_words", align_bytes=64)
+        down_words = {}
         down_scales = held.tile([P, E, N], U8, name="down_scales", align_bytes=64)
         slot_scales = [held.tile([P, SLOTS], U8, name="slot_scales%d" % o, align_bytes=64) for o in range(PASSES)]
         total = held.tile([P, T], F32, name="total")
@@ -85,14 +92,22 @@ def tile_moe_res_glu_gelu_kernel(
             for r in range(4):
                 queue.dma_start(plane[r:P:32, :, :].bitcast(I32), rows[r].bitcast(I32))
 
-        def load_up_scales(m, pair, queue):
-            load_scale_rows(planes[m, pair], (w1_scales, w3_scales)[m][2 * pair : 2 * pair + 2], queue)
+        def load_up_scales(m, e0, e1):
+            load_scale_rows(planes[m, e0], (w1_scales, w3_scales)[m][e0:e1], nc.sync)
 
-        def load_gates(e0, e1):
-            tile = held.tile([P, (e1 - e0) * C], F32, name="gate%d" % e0)
-            nc.sync.dma_start(tile[:], gate[:, e0 * C : e1 * C])
+        def load_down(e0, e1):
+            tile = held.tile([P, e1 - e0, 2 * N], U8, name="down_words%d" % e0, align_bytes=64)
+            nc.sync.dma_start(tile[:].bitcast(I32), w2_words[e0:e1, 0].rearrange("e p b -> p e b").bitcast(I32))
             for e in range(e0, e1):
-                gates[e] = tile[:, (e - e0) * C : (e - e0 + 1) * C]
+                down_words[e] = tile[:, e - e0, :]
+
+        def load_gates(t0, t1):
+            gates[t0] = held.tile([P, (t1 - t0) * P], F32, name="gate%d" % t0)
+            nc.sync.dma_start(gates[t0][:], gate[:, t0 * P : t1 * P])
+
+        def gate_of(t, width):
+            t0 = max(s for s in gates if s <= t)
+            return gates[t0][:, (t - t0) * P : (t - t0) * P + width]
 
         def part_list(e0, e1):
             return offsets[:, e0 * LIST_COLS : e1 * LIST_COLS]
@@ -124,7 +139,7 @@ def tile_moe_res_glu_gelu_kernel(
                 lhsT=slot_words[o, t].bitcast(FP8X4),
                 lhsT_scale=slot_scales[o][:, t * P : (t + 1) * P],
                 rhs=up_words[m, e, o].bitcast(FP4X4),
-                rhs_scale=planes[m, e // 2][:, (e % 2) * PASSES + o, :],
+                rhs_scale=up_scales[m, e, o],
                 start=(o == 0),
                 stop=(o == PASSES - 1),
             )
@@ -142,47 +157,55 @@ def tile_moe_res_glu_gelu_kernel(
                 hidden[t] = held.tile([P, 2, P, 2], BF16, name=name, tag=tag or name, align_bytes=64)
                 nc.vector.tensor_tensor(hidden[t][:], by_pairs(sums[m, t]), act[t][:], MULT)
 
-        def up(m, t, bank):
+        def up(m, t, bank, tag=None):
             up_pass(m, t, 0, bank)
-            finish(m, t)
+            finish(m, t, tag)
 
-        def turn(tiles, bank):
-            e = tiles[0] // TILES
+        def turn(tiles, bank, on_scalar):
+            first = tiles[0]
             turned = bank[:, 0 : len(tiles) * 2 * P].rearrange("p (j u c) -> p j u c", u=2, c=P)
             for j, t in enumerate(tiles):
                 pairs = hidden[t][:].rearrange("c u p v -> c (u p v)").bitcast(F32)
                 for u in range(2):
                     nc.tensor.transpose(turned[:, j, u, :], pairs[:, u * P : (u + 1) * P], ident[:])
-            if e not in h_t:
-                h_t[e] = held.tile([P, 4 * C], BF16, name="h_t%d" % e, align_bytes=64)
-            first = tiles[0] - e * TILES
-            words = h_t[e][:].bitcast(F32).rearrange("p (j c u) -> p j c u", j=TILES, u=2)
-            nc.scalar.copy(words[:, first : first + len(tiles)], turned.rearrange("p j u c -> p j c u"))
+            h_t[first] = held.tile([P, 4 * P * len(tiles)], BF16, name="h_t%d" % first, align_bytes=64)
+            words = h_t[first][:].bitcast(F32).rearrange("p (j c u) -> p j c u", j=len(tiles), u=2)
+            if on_scalar:
+                nc.scalar.copy(words, turned.rearrange("p j u c -> p j c u"))
+            else:
+                nc.vector.tensor_copy(words, turned.rearrange("p j u c -> p j c u"))
 
-        def quantize(e):
-            h_words[e] = held.tile([P, C], U32, name="h_words%d" % e, align_bytes=64)
-            h_scales[e] = held.tile([P, C], U8, name="h_scales%d" % e, align_bytes=64)
-            nc.vector.quantize_mx(out=h_words[e][:].bitcast(FP8X4), scales=h_scales[e][:], in_=h_t[e][:])
+        def quantize(tiles):
+            first, width = tiles[0], len(tiles) * P
+            h_words[first] = held.tile([P, width], U32, name="h_words%d" % first, align_bytes=64)
+            h_scales[first] = held.tile([P, width], U8, name="h_scales%d" % first, align_bytes=64)
+            nc.vector.quantize_mx(out=h_words[first][:].bitcast(FP8X4), scales=h_scales[first][:], in_=h_t[first][:])
 
-        def down(e, bank):
-            y = bank[:, 0:C]
+        def down(tiles, bank):
+            first, width = tiles[0], len(tiles) * P
+            e = first // TILES
+            y = bank[:, 0:width]
             nc.tensor.matmul_mx(
                 out=y,
-                lhsT=down_words[:, e, :].bitcast(FP4X4),
+                lhsT=down_words[e].bitcast(FP4X4),
                 lhsT_scale=down_scales[:, e, :],
-                rhs=h_words[e][:].bitcast(FP8X4),
-                rhs_scale=h_scales[e][:],
+                rhs=h_words[first][:].bitcast(FP8X4),
+                rhs_scale=h_scales[first][:],
                 start=True,
                 stop=True,
             )
-            y_sb[e] = held.tile([P, C], F32, name="y_sb%d" % e)
-            nc.scalar.copy(y_sb[e][:], y)
-            nc.vector.tensor_tensor(routed[:].indirect(part_list(e, e + 1)), y_sb[e][:], gates[e], MULT)
+            if e not in y_sb:
+                y_sb[e] = held.tile([P, C], F32, name="y_sb%d" % e)
+            cols = slice((first - e * TILES) * P, (first - e * TILES) * P + width)
+            nc.vector.tensor_tensor(y_sb[e][:, cols], y, gate_of(first, width), MULT)
+
+        def scatter(e):
+            nc.scalar.activation(routed[:].indirect(part_list(e, e + 1)), y_sb[e][:], COPY)
 
         for plane in (tok_scales, down_scales):
             zero_bytes(nc.gpsimd, plane)
         nc.vector.memset(zero[:], 0.0)
-        for plane in (planes[W1, 0], slot_scales[1], planes[W3, 0], planes[W1, 1], planes[W3, 1]):
+        for plane in (planes[W1, 0], slot_scales[1], planes[W3, 0], planes[W1, 2], planes[W3, 2]):
             zero_bytes(nc.vector, plane)
         make_identity(nc, ident[:])
 
@@ -193,23 +216,23 @@ def tile_moe_res_glu_gelu_kernel(
         load_scale_rows(down_scales, w2_scales, nc.gpsimd)
         for pair in range(2):
             gather_scales(pair)
-        load_up_scales(W1, 0, nc.sync)
+        load_up_scales(W1, 0, 2)
         load_tokens(1)
         move_scales(0)
         load_up(W1, (0, 1), (1,))
-        load_up_scales(W3, 0, nc.sync)
+        load_up_scales(W3, 0, 2)
         load_up(W3, (0,), (0, 1))
         load_up(W3, (1,), (0, 1))
         move_scales(1)
         load_up(W1, (2,), (0, 1))
-        load_up_scales(W1, 1, nc.sync)
+        load_up_scales(W1, 2, 4)
         load_up(W3, (2,), (0, 1))
-        load_up_scales(W3, 1, nc.sync)
-        nc.sync.dma_start(down_words[:].bitcast(I32), w2_words.rearrange("e s p b -> p (e s) b").bitcast(I32))
+        load_up_scales(W3, 2, 4)
+        load_down(0, E)
+        load_gates(0, 2)
         load_up(W1, (3,), (0, 1))
-        load_gates(0, 1)
         load_up(W3, (3,), (0, 1))
-        load_gates(1, E)
+        load_gates(2, 8)
         nc.sync.dma_start(total[:], xr)
 
         for e in range(3):
@@ -224,26 +247,33 @@ def tile_moe_res_glu_gelu_kernel(
         for t in range(4):
             up(W3, t, banks[4 + t])
         gather_words(0, 3, 4, tag="up1_1_0")
-        turn((0, 1), banks[0])
-        quantize(0)
+        turn((0, 1), banks[0], True)
+        quantize((0, 1))
         up(W1, 4, banks[1])
         up(W1, 5, banks[2])
         up(W3, 4, banks[3])
         up(W3, 5, banks[5])
-        down(0, banks[4])
+        down((0, 1), banks[4])
+        scatter(0)
+        turn((2, 3), banks[3], False)
+        quantize((2, 3))
         up(W1, 6, banks[6])
-        turn((2, 3), sums[W3, 4])
-        turn((4, 5), sums[W3, 5])
-        quantize(1)
-        quantize(2)
+        turn((4, 5), banks[0], False)
+        quantize((4, 5))
         up(W1, 7, banks[7])
-        up(W3, 6, banks[0])
-        up(W3, 7, banks[1])
-        down(1, banks[2])
-        turn((6, 7), banks[6])
-        quantize(3)
-        down(2, sums[W3, 7])
-        down(3, banks[4])
+        down((2, 3), banks[1])
+        scatter(1)
+        up(W3, 6, banks[2])
+        up(W3, 7, banks[4])
+        down((4, 5), banks[5])
+        turn((6,), banks[3], False)
+        quantize((6,))
+        turn((7,), banks[6], False)
+        quantize((7,))
+        scatter(2)
+        down((6,), banks[0])
+        down((7,), banks[7])
+        scatter(3)
 
         for c0, c1 in zip(OUT_CUTS, OUT_CUTS[1:]):
             cols = slice(c0, c1)

from contextlib import ExitStack

import concourse.mybir as mybir
from concourse.masks import make_identity

K, T, E, C, H, N = 1024, 2048, 4, 256, 512, 128
SLOTS = E * C
FLOPS = 2 * SLOTS * H * (2 * K + N)

F32 = mybir.dt.float32
BF16 = mybir.dt.bfloat16
I32 = mybir.dt.int32
U32 = mybir.dt.uint32
U16 = mybir.dt.uint16
U8 = mybir.dt.uint8
FP8X4 = mybir.dt.float8_e4m3fn_x4
FP4X4 = mybir.dt.float4_e2m1fn_x4
MULT = mybir.AluOpType.mult
ADD = mybir.AluOpType.add
GELU = mybir.ActivationFunctionType.Gelu_apprx_tanh
COPY = mybir.ActivationFunctionType.Copy

P = 128
PASSES = K // 512
TILES = C // P
LIST_COLS = C // 16
BANKS = 8
OUT_CUTS = (0, 256, 768, 1280, 1792, 2048)
LIVE_ROWS = 100
SHIFT = 16
W1, W3 = 0, 1
SCALE_GROUPS = ((W1, 0, 2), (W3, 0, 2), (W1, 2, 4), (W3, 2, 4))


def tile_moe_res_glu_gelu_kernel(
    tc, x_words, x_scales, xr, w1_words, w1_scales, w3_words, w3_scales, w2_words, w2_scales, gate, offs, out
):
    nc = tc.nc
    with ExitStack() as ctx:
        held = ctx.enter_context(tc.tile_pool(name="held", bufs=1))
        psum = ctx.enter_context(tc.psum_pool(name="psum", bufs=1))

        offsets = held.tile([P, SLOTS // 16], U16, name="offsets")
        nc.sync.dma_start(offsets[:], offs)

        tok_words = [held.tile([P, T], I32, name="tok_words%d" % o) for o in range(PASSES)]
        tok_scales = held.tile([P, T], U8, name="tok_scales")
        planes = {
            (m, e0): held.tile([P, (e1 - e0) * PASSES, H], U8, name="planes%d_%d" % (m, e0), align_bytes=64)
            for m, e0, e1 in SCALE_GROUPS
        }
        up_scales = {
            (m, e, o): planes[m, e0][:, (e - e0) * PASSES + o, :]
            for m, e0, e1 in SCALE_GROUPS
            for e in range(e0, e1)
            for o in range(PASSES)
        }
        zero = held.tile([P, 1], F32, name="zero")
        down_words = {}
        down_scales = held.tile([P, E, N], U8, name="down_scales", align_bytes=64)
        slot_scales = [held.tile([P, SLOTS], U8, name="slot_scales%d" % o, align_bytes=64) for o in range(PASSES)]
        total = held.tile([P, T], F32, name="total")
        routed = held.tile([P, T], F32, name="routed")
        ident = held.tile([P, P], F32, name="ident")
        banks = [psum.tile([P, H], F32, name="bank%d" % b) for b in range(BANKS)]
        up_words, slot_words, gates, sums, act, hidden, h_t, h_words, h_scales, y_sb = {}, {}, {}, {}, {}, {}, {}, {}, {}, {}
        def zero_bytes(engine, tile):
            engine.memset(tile[:].bitcast(I32), 0)

        def load_tokens(o):
            nc.sync.dma_start(tok_words[o][:], x_words[o].rearrange("p t r -> p (t r)").bitcast(I32))

        def load_token_scales():
            rows = x_scales.rearrange("o (q r) t -> r q o t", r=4)
            for r in range(4):
                nc.sync.dma_start(tok_scales[r:P:SHIFT, :].bitcast(I32), rows[r].bitcast(I32))

        def load_up(m, experts, passes):
            src = (w1_words, w3_words)[m][experts[0] : experts[-1] + 1, passes[0] : passes[-1] + 1]
            name = "up%d_%d_%d" % (m, experts[0], passes[0])
            tile = held.tile([P, len(experts) * len(passes), 2 * H], U8, name=name, align_bytes=64)
            if len(passes) == 1:
                src = src[:, 0].rearrange("e p b -> p e b")
            else:
                src = src[0].rearrange("s p b -> p s b")
            nc.sync.dma_start(tile[:].bitcast(I32), src.bitcast(I32))
            for i, key in enumerate((m, e, o) for e in experts for o in passes):
                up_words[key] = tile[:, i, :]

        def load_scale_rows(plane, scales, queue):
            rows = scales.rearrange("e s (q r) n -> r q (e s) n", r=4)
            for r in range(4):
                queue.dma_start(plane[r:P:32, :, :].bitcast(I32), rows[r].bitcast(I32))

        def load_up_scales(m, e0, e1):
            load_scale_rows(planes[m, e0], (w1_scales, w3_scales)[m][e0:e1], nc.sync)

        def load_down(e0, e1):
            tile = held.tile([P, e1 - e0, 2 * N], U8, name="down_words%d" % e0, align_bytes=64)
            nc.sync.dma_start(tile[:].bitcast(I32), w2_words[e0:e1, 0].rearrange("e p b -> p e b").bitcast(I32))
            for e in range(e0, e1):
                down_words[e] = tile[:, e - e0, :]

        def load_gates(t0, t1):
            gates[t0] = held.tile([P, (t1 - t0) * P], F32, name="gate%d" % t0)
            nc.sync.dma_start(gates[t0][:], gate[:, t0 * P : t1 * P])

        def gate_of(t, width):
            t0 = max(s for s in gates if s <= t)
            return gates[t0][:, (t - t0) * P : (t - t0) * P + width]

        def part_list(e0, e1):
            return offsets[:, e0 * LIST_COLS : e1 * LIST_COLS]

        def gather_words(o, e0, e1, tag=None):
            name = "slot_words%d_%d" % (o, e0)
            tile = held.tile([P, (e1 - e0) * C], U32, name=name, tag=tag or name, align_bytes=64)
            nc.vector.tensor_copy(tile[:], tok_words[o][:].bitcast(U32).indirect(part_list(e0, e1)))
            for t in range(e0 * TILES, e1 * TILES):
                slot_words[o, t] = tile[:, (t - e0 * TILES) * P : (t - e0 * TILES + 1) * P]

        def gather_scales(pair):
            cols = slice(pair * 2 * C, (pair + 1) * 2 * C)
            nc.vector.tensor_copy(slot_scales[0][:, cols], tok_scales[:].indirect(part_list(2 * pair, 2 * pair + 2)))

        def move_scales(pair):
            cols = slice(pair * 2 * C, (pair + 1) * 2 * C)
            nc.sync.dma_start(
                slot_scales[1][0:LIVE_ROWS, cols].bitcast(I32),
                slot_scales[0][SHIFT : SHIFT + LIVE_ROWS, cols].bitcast(I32),
            )

        def up_pass(m, t, o, bank=None):
            e = t // TILES
            if o == 0:
                sums[m, t] = bank
            nc.tensor.matmul_mx(
                out=sums[m, t][:],
                lhsT=slot_words[o, t].bitcast(FP8X4),
                lhsT_scale=slot_scales[o][:, t * P : (t + 1) * P],
                rhs=up_words[m, e, o].bitcast(FP4X4),
                rhs_scale=up_scales[m, e, o],
                start=(o == 0),
                stop=(o == PASSES - 1),
            )

        def by_pairs(bank):
            return bank[:].rearrange("c (p u v) -> c u p v", u=2, v=2)

        def finish(m, t, tag=None):
            up_pass(m, t, 1)
            if m == W1:
                act[t] = held.tile([P, 2, P, 2], F32, name="act%d" % t, align_bytes=64)
                nc.scalar.activation(act[t][:], by_pairs(sums[m, t]), GELU)
            else:
                name = "hidden%d" % t
                hidden[t] = held.tile([P, 2, P, 2], BF16, name=name, tag=tag or name, align_bytes=64)
                nc.vector.tensor_tensor(hidden[t][:], by_pairs(sums[m, t]), act[t][:], MULT)

        def up(m, t, bank, tag=None):
            up_pass(m, t, 0, bank)
            finish(m, t, tag)

        def turn(tiles, bank, on_scalar):
            first = tiles[0]
            turned = bank[:, 0 : len(tiles) * 2 * P].rearrange("p (j u c) -> p j u c", u=2, c=P)
            for j, t in enumerate(tiles):
                pairs = hidden[t][:].rearrange("c u p v -> c (u p v)").bitcast(F32)
                for u in range(2):
                    nc.tensor.transpose(turned[:, j, u, :], pairs[:, u * P : (u + 1) * P], ident[:])
            h_t[first] = held.tile([P, 4 * P * len(tiles)], BF16, name="h_t%d" % first, align_bytes=64)
            words = h_t[first][:].bitcast(F32).rearrange("p (j c u) -> p j c u", j=len(tiles), u=2)
            if on_scalar:
                nc.scalar.copy(words, turned.rearrange("p j u c -> p j c u"))
            else:
                nc.vector.tensor_copy(words, turned.rearrange("p j u c -> p j c u"))

        def quantize(tiles):
            first, width = tiles[0], len(tiles) * P
            h_words[first] = held.tile([P, width], U32, name="h_words%d" % first, align_bytes=64)
            h_scales[first] = held.tile([P, width], U8, name="h_scales%d" % first, align_bytes=64)
            nc.vector.quantize_mx(out=h_words[first][:].bitcast(FP8X4), scales=h_scales[first][:], in_=h_t[first][:])

        def down(tiles, bank):
            first, width = tiles[0], len(tiles) * P
            e = first // TILES
            y = bank[:, 0:width]
            nc.tensor.matmul_mx(
                out=y,
                lhsT=down_words[e].bitcast(FP4X4),
                lhsT_scale=down_scales[:, e, :],
                rhs=h_words[first][:].bitcast(FP8X4),
                rhs_scale=h_scales[first][:],
                start=True,
                stop=True,
            )
            if e not in y_sb:
                y_sb[e] = held.tile([P, C], F32, name="y_sb%d" % e)
            cols = slice((first - e * TILES) * P, (first - e * TILES) * P + width)
            nc.vector.tensor_tensor(y_sb[e][:, cols], y, gate_of(first, width), MULT)

        def scatter(e):
            nc.scalar.activation(routed[:].indirect(part_list(e, e + 1)), y_sb[e][:], COPY)

        for plane in (tok_scales, down_scales):
            zero_bytes(nc.gpsimd, plane)
        nc.vector.memset(zero[:], 0.0)
        for plane in (planes[W1, 0], slot_scales[1], planes[W3, 0], planes[W1, 2], planes[W3, 2]):
            zero_bytes(nc.vector, plane)
        make_identity(nc, ident[:])

        load_up(W1, (0, 1), (0,))
        load_token_scales()
        nc.scalar.activation(routed[:], zero[:].to_broadcast([P, T]), GELU)
        load_tokens(0)
        load_scale_rows(down_scales, w2_scales, nc.gpsimd)
        for pair in range(2):
            gather_scales(pair)
        load_up_scales(W1, 0, 2)
        load_tokens(1)
        move_scales(0)
        load_up(W1, (0, 1), (1,))
        load_up_scales(W3, 0, 2)
        load_up(W3, (0,), (0, 1))
        load_up(W3, (1,), (0, 1))
        move_scales(1)
        load_up(W1, (2,), (0, 1))
        load_up_scales(W1, 2, 4)
        load_up(W3, (2,), (0, 1))
        load_up_scales(W3, 2, 4)
        load_down(0, E)
        load_gates(0, 2)
        load_up(W1, (3,), (0, 1))
        load_up(W3, (3,), (0, 1))
        load_gates(2, 8)
        nc.sync.dma_start(total[:], xr)

        for e in range(3):
            gather_words(0, e, e + 1)
        for e in range(E):
            gather_words(1, e, e + 1)

        for t in range(4):
            up_pass(W1, t, 0, banks[t])
        for t in range(4):
            finish(W1, t)
        for t in range(4):
            up(W3, t, banks[4 + t])
        gather_words(0, 3, 4, tag="up1_1_0")
        turn((0, 1), banks[0], True)
        quantize((0, 1))
        up(W1, 4, banks[1])
        up(W1, 5, banks[2])
        up(W3, 4, banks[3])
        up(W3, 5, banks[5])
        down((0, 1), banks[4])
        scatter(0)
        turn((2, 3), banks[3], False)
        quantize((2, 3))
        up(W1, 6, banks[6])
        turn((4, 5), banks[0], False)
        quantize((4, 5))
        up(W1, 7, banks[7])
        down((2, 3), banks[1])
        scatter(1)
        up(W3, 6, banks[2])
        up(W3, 7, banks[4])
        down((4, 5), banks[5])
        turn((6,), banks[3], False)
        quantize((6,))
        turn((7,), banks[6], False)
        quantize((7,))
        scatter(2)
        down((6,), banks[0])
        down((7,), banks[7])
        scatter(3)

        for c0, c1 in zip(OUT_CUTS, OUT_CUTS[1:]):
            cols = slice(c0, c1)
            nc.vector.tensor_tensor(total[:, cols], routed[:, cols], total[:, cols], ADD)
            nc.sync.dma_start(out[:, cols], total[:, cols])
